import numpy as np
import ml_dtypes


def mxq(x, axis, fmt="e4m3"):
    dtype, down = {"e4m3": (ml_dtypes.float8_e4m3fn, 7), "e5m2": (ml_dtypes.float8_e5m2, 14)}[fmt]
    v = np.moveaxis(np.asarray(x, np.float32).astype(ml_dtypes.bfloat16).astype(np.float64), axis, -1)
    blocks = v.reshape(v.shape[:-1] + (-1, 32))
    amax = np.abs(blocks).max(-1, keepdims=True)
    byte = np.maximum(np.where(amax > 0, np.frexp(amax)[1] - 1 + 127, 0) - down, 1)
    scale = np.exp2(byte - 127.0)
    codes = (blocks / scale).astype(np.float32).astype(dtype).astype(np.float64)
    return np.moveaxis((codes * scale).reshape(v.shape), -1, axis)


WIDE = False


def mx_kscale(k):
    if not WIDE:
        return np.ones(k)
    levels = np.array([10, -10, 5, -5, 0])
    if k % 512:
        return np.exp2(np.random.permutation(np.resize(levels, k // 32))).repeat(32)
    a = np.empty((k // 512, 16))
    for p in range(k // 512):
        a[p, :8] = np.random.permutation(np.resize(levels, 8))
        for g in range(8):
            far = levels[np.abs(levels - a[p, g]) >= 10]
            a[p, g + 8] = far[np.random.randint(len(far))]
    return np.exp2(a.ravel()).repeat(32)


def f64(x):
    return np.asarray(x).astype(np.float64)


def striped(idx):
    return np.tile(idx.reshape(-1, 16).T, (8, 1)).astype(np.uint16)


def unstriped(offs):
    return offs[:16].T.reshape(-1).astype(np.int64)


def pack_weight(w):
    k, n = w.shape
    w = f64(np.asarray(w, np.float32).astype(ml_dtypes.bfloat16)).reshape(k // 32, 32, n)
    amax = np.abs(w).max(1)
    byte = np.clip(np.where(amax > 0, np.frexp(amax)[1] - 1 + 127 - 7, 1), 1, 254)
    scaled = (w * np.exp2(127.0 - byte)[:, None, :]).reshape(k, n).astype(np.float32)
    words = np.ascontiguousarray(scaled.reshape(k // 512, 128, 4, n).transpose(0, 1, 3, 2)).astype(ml_dtypes.float8_e4m3fn).view(np.uint8)
    return words, np.ascontiguousarray(byte.astype(np.uint8).reshape(k // 512, 16, n))


def unpack_weight(words, scales):
    g, p, n, _ = words.shape
    vals = np.ascontiguousarray(words).view(ml_dtypes.float8_e4m3fn).astype(np.float64) * np.repeat(np.exp2(scales.astype(np.float64) - 127.0), 8, axis=1)[..., None]
    return vals.transpose(0, 1, 3, 2).reshape(g * 512, n)


def sigmoid(v):
    return 1.0 / (1.0 + np.exp(-np.maximum(v, -700.0)))


K, T, S, V, N = 512, 4096, 1024, 512, 256


def setup_inputs():
    n = np.random.standard_normal
    s = mx_kscale(K)[:, None]
    packed_w1 = pack_weight(n((K, N)) / np.sqrt(K) / s)
    packed_w2 = pack_weight(n((K, N)) / np.sqrt(K) / s)
    packed_w3 = pack_weight(n((K, N)) / np.sqrt(K) / s)
    return {
        "xT": (n((K, T)) * s).astype(np.float32),
        "w1_words": packed_w1[0],
        "w1_scales": packed_w1[1],
        "w2_words": packed_w2[0],
        "w2_scales": packed_w2[1],
        "w3_words": packed_w3[0],
        "w3_scales": packed_w3[1],
        "offs": striped(np.random.permutation(T)[:S]),
        "cen": striped(np.random.permutation(S)[:V]),
        "pos1": striped(np.random.permutation(S)[:V]),
        "pos2": striped(np.random.permutation(S)[:V]),
    }


def reference(xT, w1_words, w1_scales, w2_words, w2_scales, w3_words, w3_scales, offs, cen, pos1, pos2):
    xq = mxq(f64(xT)[:, unstriped(offs)], 0, "e4m3")
    y = unpack_weight(w1_words, w1_scales).T @ xq
    yc = y[:, unstriped(cen)]
    e = unpack_weight(w2_words, w2_scales).T @ xq
    h = unpack_weight(w3_words, w3_scales).T @ xq
    z = (sigmoid(yc + e[:, unstriped(pos1)])) * h[:, unstriped(pos1)] + (sigmoid(yc + e[:, unstriped(pos2)])) * h[:, unstriped(pos2)]
    return z

@@ -1,0 +1,144 @@
+from contextlib import ExitStack
+
+import concourse.mybir as mybir
+
+K, T, S, V, N = 512, 4096, 1024, 512, 256
+FLOPS = 3 * 2 * K * N * S
+
+F32 = mybir.dt.float32
+BF16 = mybir.dt.bfloat16
+I32 = mybir.dt.int32
+U32 = mybir.dt.uint32
+U16 = mybir.dt.uint16
+U8 = mybir.dt.uint8
+FP8X4 = mybir.dt.float8_e4m3fn_x4
+ADD = mybir.AluOpType.add
+MULT = mybir.AluOpType.mult
+COPY = mybir.ActivationFunctionType.Copy
+SIGMOID = mybir.ActivationFunctionType.Sigmoid
+
+P = 128
+PACK = 4
+HALF = S // 2
+LAST_CHUNKS = ((0, 1024, "scalar"), (1024, 2048, "scalar"), (2048, 3072, "vector"), (3072, 3840, "vector"), (3840, 4096, "scalar"))
+
+
+def tile_picked_gatedg_none_e_kernel(
+    tc, xT, w1_words, w1_scales, w2_words, w2_scales, w3_words, w3_scales, offs, cen, pos1, pos2, out
+):
+    nc = tc.nc
+    with ExitStack() as ctx:
+        keep = ctx.enter_context(tc.tile_pool(name="keep", bufs=1))
+        psum = ctx.enter_context(tc.psum_pool(name="psum", bufs=1))
+
+        offs_sb = keep.tile([P, S // 16], U16, name="offs_sb")
+        cen_sb = keep.tile([P, V // 16], U16, name="cen_sb")
+        pos_sb = [keep.tile([P, V // 16], U16, name="pos%d_sb" % d) for d in range(2)]
+
+        rows = xT.rearrange("(p j) t -> p j t", j=PACK)
+        plane = [keep.tile([P, T], F32, name="plane%d" % j) for j in range(PACK)]
+        last_bf = keep.tile([P, T], BF16, name="last_bf")
+
+        warm_in = keep.tile([P, 1], F32, name="warm_in")
+        warm_out = keep.tile([P, 1], F32, name="warm_out")
+        nc.vector.memset(warm_in[:], 0.0)
+        nc.scalar.activation(warm_out[:], warm_in[:], SIGMOID)
+
+        nc.sync.dma_start(plane[0][:], rows[:, 0, :])
+        nc.sync.dma_start(offs_sb[:], offs)
+        nc.sync.dma_start(plane[1][:], rows[:, 1, :])
+        nc.sync.dma_start(plane[2][:], rows[:, 2, :])
+        for c0, c1, eng in LAST_CHUNKS:
+            nc.sync.dma_start(plane[3][:, c0:c1], rows[:, 3, c0:c1])
+
+        w_words = []
+        w_scales = []
+        for i, (words, scales) in enumerate(((w1_words, w1_scales), (w2_words, w2_scales), (w3_words, w3_scales))):
+            wt = keep.tile([P, N], U32, name="w_words%d" % i, align_bytes=64)
+            nc.sync.dma_start(wt[:].bitcast(I32), words[0].rearrange("p n t -> p (n t)").bitcast(I32))
+            st = keep.tile([P, N], U8, name="w_scales%d" % i, align_bytes=64)
+            nc.gpsimd.memset(st[:], 0)
+            for q in range(4):
+                nc.gpsimd.dma_start(st[32 * q : 32 * q + 4, :].bitcast(I32), scales[0, 4 * q : 4 * q + 4, :].bitcast(I32))
+            w_words.append(wt)
+            w_scales.append(st)
+        nc.sync.dma_start(cen_sb[:], cen)
+        nc.sync.dma_start(pos_sb[0][:], pos1)
+        nc.sync.dma_start(pos_sb[1][:], pos2)
+
+        picked = [keep.tile([P, HALF, PACK], BF16, name="picked%d" % h, align_bytes=64) for h in range(2)]
+        lists = [offs_sb[:, h * (HALF // 16) : (h + 1) * (HALF // 16)] for h in range(2)]
+        for j in range(PACK - 1):
+            for h in range(2):
+                nc.vector.tensor_copy(picked[h][:, :, j], plane[j][:].indirect(lists[h]))
+        for c0, c1, eng in LAST_CHUNKS:
+            if eng == "scalar":
+                nc.scalar.activation(last_bf[:, c0:c1], plane[3][:, c0:c1], COPY)
+            else:
+                nc.vector.tensor_copy(last_bf[:, c0:c1], plane[3][:, c0:c1])
+        nc.vector.tensor_copy(picked[0][:, :, 3], plane[3][:].indirect(lists[0]))
+        nc.scalar.activation(picked[1][:, :, 3], last_bf[:].indirect(lists[1]), COPY)
+
+        codes = [keep.tile([P, HALF], U32, name="codes%d" % h, align_bytes=64) for h in range(2)]
+        xsc = [keep.tile([P, HALF], U8, name="xsc%d" % h, align_bytes=64) for h in range(2)]
+        for h in range(2):
+            nc.vector.quantize_mx(
+                out=codes[h][:].bitcast(FP8X4), scales=xsc[h][:], in_=picked[h][:].rearrange("p n j -> p (n j)")
+            )
+
+        res = [[keep.tile([P, S], F32, name="res%d_%d" % (b, i)) for i in range(3)] for b in range(2)]
+
+        def product(b, i, h, bank, on_vector):
+            acc = psum.tile([P, HALF], F32, name="acc", tag="bank%d" % bank)
+            cols = slice(b * P, (b + 1) * P)
+            nc.tensor.matmul_mx(
+                out=acc[:],
+                lhsT=w_words[i][:, cols].bitcast(FP8X4),
+                lhsT_scale=w_scales[i][:, cols],
+                rhs=codes[h][:].bitcast(FP8X4),
+                rhs_scale=xsc[h][:],
+                start=True,
+                stop=True,
+            )
+            dst = res[b][i][:, h * HALF : (h + 1) * HALF]
+            if on_vector:
+                nc.vector.tensor_copy(dst, acc[:])
+            else:
+                nc.scalar.activation(dst, acc[:], COPY)
+
+        product(0, 0, 0, 0, False)
+        product(0, 0, 1, 1, True)
+        product(0, 1, 0, 2, False)
+        product(0, 1, 1, 3, False)
+        product(0, 2, 0, 1, False)
+        product(0, 2, 1, 4, False)
+
+        def later_products():
+            product(1, 0, 0, 3, False)
+            product(1, 0, 1, 5, False)
+            product(1, 1, 0, 4, False)
+            product(1, 1, 1, 6, False)
+            product(1, 2, 0, 1, False)
+            product(1, 2, 1, 7, False)
+
+        for b in range(2):
+            y, e, hh = res[b]
+            yc = keep.tile([P, V], F32, name="yc%d" % b)
+            nc.vector.tensor_copy(yc[:], y[:].indirect(cen_sb[:]))
+            gate = []
+            for d in range(2):
+                arg = keep.tile([P, V], F32, name="arg%d_%d" % (b, d))
+                nc.vector.tensor_tensor(arg[:], e[:].indirect(pos_sb[d][:]), yc[:], ADD)
+                g = keep.tile([P, V], F32, name="gate%d_%d" % (b, d))
+                nc.scalar.activation(g[:], arg[:], SIGMOID)
+                gate.append(g)
+            if b == 0:
+                later_products()
+            term = []
+            for d in range(2):
+                t = keep.tile([P, V], F32, name="term%d_%d" % (b, d))
+                nc.vector.tensor_tensor(t[:], hh[:].indirect(pos_sb[d][:]), gate[d][:], MULT)
+                term.append(t)
+            z = keep.tile([P, V], F32, name="z%d" % b)
+            nc.vector.tensor_tensor(z[:], term[0][:], term[1][:], ADD)
+            nc.sync.dma_start(out[b * P : (b + 1) * P, :], z[:])

@@ -1,6 +1,7 @@
 from contextlib import ExitStack
 
 import concourse.mybir as mybir
+from concourse.masks import make_identity
 
 K, T, S, V, N = 512, 4096, 1024, 512, 256
 FLOPS = 3 * 2 * K * N * S
@@ -20,7 +21,9 @@ SIGMOID = mybir.ActivationFunctionType.Sigmoid
 P = 128
 PACK = 4
 HALF = S // 2
-LAST_CHUNKS = ((0, 1024, "scalar"), (1024, 2048, "scalar"), (2048, 3072, "vector"), (3072, 3840, "vector"), (3840, 4096, "scalar"))
+QUARTER = S // 4
+LAST_CHUNKS = ((0, 1792, "scalar"), (1792, 3072, "vector"), (3072, 3840, "vector"), (3840, 4096, "scalar"))
+TAIL = 128
 
 
 def tile_picked_gatedg_none_e_kernel(
@@ -44,27 +47,34 @@ def tile_picked_gatedg_none_e_kernel(
         nc.vector.memset(warm_in[:], 0.0)
         nc.scalar.activation(warm_out[:], warm_in[:], SIGMOID)
 
+        w_words = [keep.tile([P, N], U32, name="w_words%d" % i, align_bytes=64) for i in range(3)]
+        scale_tile = keep.tile([P, 3 * N], U8, name="scale_tile", align_bytes=64)
+        nc.vector.memset(scale_tile[:].bitcast(I32), 0)
+        w_scales = [scale_tile[:, i * N : (i + 1) * N] for i in range(3)]
+        words_in = (w1_words, w2_words, w3_words)
+        scales_in = (w1_scales, w2_scales, w3_scales)
+
+        def load_scales(queue, i):
+            for q in range(4):
+                queue.dma_start(w_scales[i][32 * q : 32 * q + 4, :].bitcast(I32), scales_in[i][0, 4 * q : 4 * q + 4, :].bitcast(I32))
+
         nc.sync.dma_start(plane[0][:], rows[:, 0, :])
         nc.sync.dma_start(offs_sb[:], offs)
         nc.sync.dma_start(plane[1][:], rows[:, 1, :])
+        load_scales(nc.gpsimd, 0)
+        load_scales(nc.gpsimd, 1)
+        load_scales(nc.sync, 2)
         nc.sync.dma_start(plane[2][:], rows[:, 2, :])
         for c0, c1, eng in LAST_CHUNKS:
             nc.sync.dma_start(plane[3][:, c0:c1], rows[:, 3, c0:c1])
-
-        w_words = []
-        w_scales = []
-        for i, (words, scales) in enumerate(((w1_words, w1_scales), (w2_words, w2_scales), (w3_words, w3_scales))):
-            wt = keep.tile([P, N], U32, name="w_words%d" % i, align_bytes=64)
-            nc.sync.dma_start(wt[:].bitcast(I32), words[0].rearrange("p n t -> p (n t)").bitcast(I32))
-            st = keep.tile([P, N], U8, name="w_scales%d" % i, align_bytes=64)
-            nc.gpsimd.memset(st[:], 0)
-            for q in range(4):
-                nc.gpsimd.dma_start(st[32 * q : 32 * q + 4, :].bitcast(I32), scales[0, 4 * q : 4 * q + 4, :].bitcast(I32))
-            w_words.append(wt)
-            w_scales.append(st)
+        for i in range(3):
+            nc.sync.dma_start(w_words[i][:].bitcast(I32), words_in[i][0].rearrange("p n t -> p (n t)").bitcast(I32))
         nc.sync.dma_start(cen_sb[:], cen)
         nc.sync.dma_start(pos_sb[0][:], pos1)
         nc.sync.dma_start(pos_sb[1][:], pos2)
+
+        ident = keep.tile([P, P], F32, name="ident")
+        make_identity(nc, ident[:])
 
         picked = [keep.tile([P, HALF, PACK], BF16, name="picked%d" % h, align_bytes=64) for h in range(2)]
         lists = [offs_sb[:, h * (HALF // 16) : (h + 1) * (HALF // 16)] for h in range(2)]
@@ -79,66 +89,119 @@ def tile_picked_gatedg_none_e_kernel(
         nc.vector.tensor_copy(picked[0][:, :, 3], plane[3][:].indirect(lists[0]))
         nc.scalar.activation(picked[1][:, :, 3], last_bf[:].indirect(lists[1]), COPY)
 
-        codes = [keep.tile([P, HALF], U32, name="codes%d" % h, align_bytes=64) for h in range(2)]
-        xsc = [keep.tile([P, HALF], U8, name="xsc%d" % h, align_bytes=64) for h in range(2)]
-        for h in range(2):
-            nc.vector.quantize_mx(
-                out=codes[h][:].bitcast(FP8X4), scales=xsc[h][:], in_=picked[h][:].rearrange("p n j -> p (n j)")
+        codes = keep.tile([P, S], U32, name="codes", align_bytes=64)
+        xsc = keep.tile([P, S], U8, name="xsc", align_bytes=64)
+        acc = psum.tile([P, HALF], F32, name="acc", tag="bank7")
+        for n in range(5):
+            nc.tensor.matmul_mx(
+                out=acc[:, 0:N],
+                lhsT=w_words[0][:, 0:P].bitcast(FP8X4),
+                lhsT_scale=w_scales[0][:, 0:P],
+                rhs=w_words[0][:].bitcast(FP8X4),
+                rhs_scale=w_scales[0],
+                start=(n == 0),
+                stop=(n == 4),
             )
 
-        res = [[keep.tile([P, S], F32, name="res%d_%d" % (b, i)) for i in range(3)] for b in range(2)]
+        res = [[keep.tile([P, S], F32, name="res0_%d" % i) for i in range(3)], [None] * 3]
 
-        def product(b, i, h, bank, on_vector):
+        def x_scales(c0, c1):
+            if c0 >= S - 128:
+                return scale_tile[4:P, N + c0 - (S - 128) : N + c1 - (S - 128)]
+            return xsc[:, c0:c1]
+
+        def quantize(c0, c1):
+            h = c0 // HALF
+            nc.vector.quantize_mx(
+                out=codes[:, c0:c1].bitcast(FP8X4),
+                scales=x_scales(c0, c1),
+                in_=picked[h][:, c0 - h * HALF : c1 - h * HALF, :].rearrange("p n j -> p (n j)"),
+            )
+
+        def product(b, i, cuts, bank, on_vector):
+            c0, c1 = cuts[0], cuts[-1]
             acc = psum.tile([P, HALF], F32, name="acc", tag="bank%d" % bank)
             cols = slice(b * P, (b + 1) * P)
-            nc.tensor.matmul_mx(
-                out=acc[:],
-                lhsT=w_words[i][:, cols].bitcast(FP8X4),
-                lhsT_scale=w_scales[i][:, cols],
-                rhs=codes[h][:].bitcast(FP8X4),
-                rhs_scale=xsc[h][:],
-                start=True,
-                stop=True,
-            )
-            dst = res[b][i][:, h * HALF : (h + 1) * HALF]
+            for a0, a1 in zip(cuts[:-1], cuts[1:]):
+                nc.tensor.matmul_mx(
+                    out=acc[:, a0 - c0 : a1 - c0],
+                    lhsT=w_words[i][:, cols].bitcast(FP8X4),
+                    lhsT_scale=w_scales[i][:, cols],
+                    rhs=codes[:, a0:a1].bitcast(FP8X4),
+                    rhs_scale=x_scales(a0, a1),
+                    start=True,
+                    stop=True,
+                )
+            dst = res[b][i][:, c0:c1]
             if on_vector:
-                nc.vector.tensor_copy(dst, acc[:])
+                nc.vector.tensor_copy(dst, acc[:, 0 : c1 - c0])
             else:
-                nc.scalar.activation(dst, acc[:], COPY)
+                nc.scalar.activation(dst, acc[:, 0 : c1 - c0], COPY)
 
-        product(0, 0, 0, 0, False)
-        product(0, 0, 1, 1, True)
-        product(0, 1, 0, 2, False)
-        product(0, 1, 1, 3, False)
-        product(0, 2, 0, 1, False)
-        product(0, 2, 1, 4, False)
+        for c0, c1 in ((0, 256), (256, 512), (512, 768), (768, 896), (896, 1024)):
+            quantize(c0, c1)
+        product(0, 0, (0, 256, 512), 0, False)
+        product(0, 0, (512, 768), 1, False)
+        product(0, 0, (768, 896), 2, True)
+        product(0, 0, (896, 1024), 3, True)
+        product(0, 1, (0, 256), 4, False)
+        product(0, 1, (256, 512), 5, False)
+        product(0, 1, (512, 768), 6, False)
+        product(0, 1, (768, 896, 1024), 7, False)
+        product(0, 2, (0, 512), 4, False)
+        product(0, 2, (512, 768, 896, 1024), 5, False)
 
         def later_products():
-            product(1, 0, 0, 3, False)
-            product(1, 0, 1, 5, False)
-            product(1, 1, 0, 4, False)
-            product(1, 1, 1, 6, False)
-            product(1, 2, 0, 1, False)
-            product(1, 2, 1, 7, False)
+            res[1][0] = keep.tile([P, S], F32, name="res1_0", tag="arg0_0")
+            res[1][1] = keep.tile([P, S], F32, name="res1_1", tag="arg0_1")
+            res[1][2] = keep.tile([P, S], F32, name="res1_2", tag="yc0")
+            product(1, 0, (0, 512), 6, False)
+            product(1, 0, (512, 768, 896, 1024), 7, False)
+            product(1, 1, (0, 512), 4, False)
+            product(1, 1, (512, 768, 896, 1024), 5, False)
+            product(1, 2, (0, 512), 6, False)
+            product(1, 2, (512, 768, 896, 1024), 7, False)
 
         for b in range(2):
             y, e, hh = res[b]
-            yc = keep.tile([P, V], F32, name="yc%d" % b)
+            yc = keep.tile([P, V], F32, name="yc%d" % b, tag="yc%d" % b)
             nc.vector.tensor_copy(yc[:], y[:].indirect(cen_sb[:]))
+
             gate = []
             for d in range(2):
-                arg = keep.tile([P, V], F32, name="arg%d_%d" % (b, d))
+                arg = keep.tile([P, V], F32, name="arg%d_%d" % (b, d), tag="arg%d_%d" % (b, d))
                 nc.vector.tensor_tensor(arg[:], e[:].indirect(pos_sb[d][:]), yc[:], ADD)
                 g = keep.tile([P, V], F32, name="gate%d_%d" % (b, d))
                 nc.scalar.activation(g[:], arg[:], SIGMOID)
                 gate.append(g)
             if b == 0:
                 later_products()
-            term = []
-            for d in range(2):
-                t = keep.tile([P, V], F32, name="term%d_%d" % (b, d))
-                nc.vector.tensor_tensor(t[:], hh[:].indirect(pos_sb[d][:]), gate[d][:], MULT)
-                term.append(t)
+            term = [keep.tile([P, V], F32, name="term%d_%d" % (b, d)) for d in range(2)]
+            nc.vector.tensor_tensor(term[0][:], hh[:].indirect(pos_sb[0][:]), gate[0][:], MULT)
+
             z = keep.tile([P, V], F32, name="z%d" % b)
-            nc.vector.tensor_tensor(z[:], term[0][:], term[1][:], ADD)
-            nc.sync.dma_start(out[b * P : (b + 1) * P, :], z[:])
+            pieces = ((0, V),) if b == 0 else ((0, V - TAIL), (V - TAIL, V))
+            for v0, v1 in pieces:
+                nc.vector.tensor_tensor(
+                    term[1][:, v0:v1], hh[:].indirect(pos_sb[1][:, v0 // 16 : v1 // 16]), gate[1][:, v0:v1], MULT
+                )
+            if b == 0:
+                turned = psum.tile([P, V], F32, name="acc", tag="bank0")
+                for c in range(V // P):
+                    for d in range(2):
+                        nc.tensor.matmul(
+                            turned[:, c * P : (c + 1) * P], term[d][:, c * P : (c + 1) * P], ident[:],
+                            is_transpose=True, start=(d == 0), stop=(d == 1),
+                        )
+                turned_sb = keep.tile([P, V], F32, name="turned_sb")
+                nc.scalar.activation(turned_sb[:], turned[:], COPY)
+                back = psum.tile([P, V], F32, name="acc", tag="bank1")
+                for c in range(V // P):
+                    nc.tensor.transpose(back[:, c * P : (c + 1) * P], turned_sb[:, c * P : (c + 1) * P], ident[:])
+                nc.scalar.activation(z[:], back[:], COPY)
+                nc.sync.dma_start(out[0:P, :], z[:])
+                continue
+
+            for v0, v1 in pieces:
+                nc.vector.tensor_tensor(z[:, v0:v1], term[0][:, v0:v1], term[1][:, v0:v1], ADD)
+                (nc.sync if v0 == 0 else nc.scalar).dma_start(out[b * P : (b + 1) * P, v0:v1], z[:, v0:v1])

@@ -48,15 +48,20 @@ def tile_picked_gatedg_none_e_kernel(
         nc.scalar.activation(warm_out[:], warm_in[:], SIGMOID)
 
         w_words = [keep.tile([P, N], U32, name="w_words%d" % i, align_bytes=64) for i in range(3)]
-        scale_tile = keep.tile([P, 3 * N], U8, name="scale_tile", align_bytes=64)
+        scale_tile = keep.tile([P, 2 * N], U8, name="scale_tile", align_bytes=64)
         nc.vector.memset(scale_tile[:].bitcast(I32), 0)
-        w_scales = [scale_tile[:, i * N : (i + 1) * N] for i in range(3)]
+        w_place = ((0, 0), (8, P), (0, N))
         words_in = (w1_words, w2_words, w3_words)
         scales_in = (w1_scales, w2_scales, w3_scales)
 
+        def w_scale(i, c0, c1):
+            r, c = w_place[i]
+            return scale_tile[r:P, c + c0 : c + c1]
+
         def load_scales(queue, i):
+            r, c = w_place[i]
             for q in range(4):
-                queue.dma_start(w_scales[i][32 * q : 32 * q + 4, :].bitcast(I32), scales_in[i][0, 4 * q : 4 * q + 4, :].bitcast(I32))
+                queue.dma_start(scale_tile[32 * q + r : 32 * q + r + 4, c : c + N].bitcast(I32), scales_in[i][0, 4 * q : 4 * q + 4, :].bitcast(I32))
 
         nc.sync.dma_start(plane[0][:], rows[:, 0, :])
         nc.sync.dma_start(offs_sb[:], offs)
@@ -92,22 +97,22 @@ def tile_picked_gatedg_none_e_kernel(
         codes = keep.tile([P, S], U32, name="codes", align_bytes=64)
         xsc = keep.tile([P, S], U8, name="xsc", align_bytes=64)
         acc = psum.tile([P, HALF], F32, name="acc", tag="bank7")
-        for n in range(5):
+        for n in range(3):
             nc.tensor.matmul_mx(
                 out=acc[:, 0:N],
                 lhsT=w_words[0][:, 0:P].bitcast(FP8X4),
-                lhsT_scale=w_scales[0][:, 0:P],
+                lhsT_scale=w_scale(0, 0, P),
                 rhs=w_words[0][:].bitcast(FP8X4),
-                rhs_scale=w_scales[0],
+                rhs_scale=w_scale(0, 0, N),
                 start=(n == 0),
-                stop=(n == 4),
+                stop=(n == 2),
             )
 
-        res = [[keep.tile([P, S], F32, name="res0_%d" % i) for i in range(3)], [None] * 3]
+        res = [[keep.tile([P, S], F32, name="res%d_%d" % (b, i)) for i in range(3)] for b in range(2)]
 
         def x_scales(c0, c1):
-            if c0 >= S - 128:
-                return scale_tile[4:P, N + c0 - (S - 128) : N + c1 - (S - 128)]
+            if c0 >= S - P:
+                return scale_tile[4:P, P + c0 - (S - P) : P + c1 - (S - P)]
             return xsc[:, c0:c1]
 
         def quantize(c0, c1):
@@ -118,15 +123,14 @@ def tile_picked_gatedg_none_e_kernel(
                 in_=picked[h][:, c0 - h * HALF : c1 - h * HALF, :].rearrange("p n j -> p (n j)"),
             )
 
-        def product(b, i, cuts, bank, on_vector):
+        def product(b, i, cuts, bank, on_vector=False):
             c0, c1 = cuts[0], cuts[-1]
             acc = psum.tile([P, HALF], F32, name="acc", tag="bank%d" % bank)
-            cols = slice(b * P, (b + 1) * P)
             for a0, a1 in zip(cuts[:-1], cuts[1:]):
                 nc.tensor.matmul_mx(
                     out=acc[:, a0 - c0 : a1 - c0],
-                    lhsT=w_words[i][:, cols].bitcast(FP8X4),
-                    lhsT_scale=w_scales[i][:, cols],
+                    lhsT=w_words[i][:, b * P : (b + 1) * P].bitcast(FP8X4),
+                    lhsT_scale=w_scale(i, b * P, (b + 1) * P),
                     rhs=codes[:, a0:a1].bitcast(FP8X4),
                     rhs_scale=x_scales(a0, a1),
                     start=True,
@@ -140,68 +144,74 @@ def tile_picked_gatedg_none_e_kernel(
 
         for c0, c1 in ((0, 256), (256, 512), (512, 768), (768, 896), (896, 1024)):
             quantize(c0, c1)
-        product(0, 0, (0, 256, 512), 0, False)
-        product(0, 0, (512, 768), 1, False)
+        product(0, 0, (0, 256, 512), 0)
+        product(0, 0, (512, 768), 1)
         product(0, 0, (768, 896), 2, True)
-        product(0, 0, (896, 1024), 3, True)
-        product(0, 1, (0, 256), 4, False)
-        product(0, 1, (256, 512), 5, False)
-        product(0, 1, (512, 768), 6, False)
-        product(0, 1, (768, 896, 1024), 7, False)
-        product(0, 2, (0, 512), 4, False)
-        product(0, 2, (512, 768, 896, 1024), 5, False)
+        product(0, 0, (896, 1024), 3)
+        low, high = (0, 512), (512, 768, 896, 1024)
+        product(1, 0, (0, 256), 4)
+        product(1, 0, (256, 512), 5)
+        product(1, 0, (512, 768), 6)
+        product(1, 0, (768, 896, 1024), 7)
+        product(0, 1, low, 0)
+        product(0, 1, high, 1)
+        product(0, 2, low, 2)
+        product(0, 2, high, 3)
 
-        def later_products():
-            res[1][0] = keep.tile([P, S], F32, name="res1_0", tag="arg0_0")
-            res[1][1] = keep.tile([P, S], F32, name="res1_1", tag="arg0_1")
-            res[1][2] = keep.tile([P, S], F32, name="res1_2", tag="yc0")
-            product(1, 0, (0, 512), 6, False)
-            product(1, 0, (512, 768, 896, 1024), 7, False)
-            product(1, 1, (0, 512), 4, False)
-            product(1, 1, (512, 768, 896, 1024), 5, False)
-            product(1, 2, (0, 512), 6, False)
-            product(1, 2, (512, 768, 896, 1024), 7, False)
-
+        yc = [keep.tile([P, V], F32, name="yc%d" % b) for b in range(2)]
         for b in range(2):
-            y, e, hh = res[b]
-            yc = keep.tile([P, V], F32, name="yc%d" % b, tag="yc%d" % b)
-            nc.vector.tensor_copy(yc[:], y[:].indirect(cen_sb[:]))
+            nc.vector.tensor_copy(yc[b][:], res[b][0][:].indirect(cen_sb[:]))
 
-            gate = []
+        gate = [[None, None], [None, None]]
+
+        def make_gate(b, d, tag):
+            arg = keep.tile([P, V], F32, name="arg%d_%d" % (b, d))
+            nc.vector.tensor_tensor(arg[:], res[b][1][:].indirect(pos_sb[d][:]), yc[b][:], ADD)
+            gate[b][d] = keep.tile([P, V], F32, name="gate%d_%d" % (b, d), tag=tag)
+            nc.scalar.activation(gate[b][d][:], arg[:], SIGMOID)
+
+        make_gate(0, 0, "gate0_0")
+        make_gate(0, 1, "gate0_1")
+        product(1, 1, low, 4)
+        product(1, 1, high, 5)
+        product(1, 2, low, 6)
+        product(1, 2, high, 7)
+
+        term = [[keep.tile([P, V], F32, name="term%d_%d" % (b, d), tag="term%d_%d" % (b, d)) for d in range(2)] for b in range(2)]
+        z = [keep.tile([P, V], F32, name="z%d" % b) for b in range(2)]
+
+        def gated(b, d, v0, v1):
+            nc.vector.tensor_tensor(
+                term[b][d][:, v0:v1], res[b][2][:].indirect(pos_sb[d][:, v0 // 16 : v1 // 16]), gate[b][d][:, v0:v1], MULT
+            )
+
+        gated(0, 0, 0, V)
+        gated(0, 1, 0, V)
+        make_gate(1, 0, "gate1_0")
+        turned = psum.tile([P, V], F32, name="acc", tag="bank0")
+        for c in range(V // P):
             for d in range(2):
-                arg = keep.tile([P, V], F32, name="arg%d_%d" % (b, d), tag="arg%d_%d" % (b, d))
-                nc.vector.tensor_tensor(arg[:], e[:].indirect(pos_sb[d][:]), yc[:], ADD)
-                g = keep.tile([P, V], F32, name="gate%d_%d" % (b, d))
-                nc.scalar.activation(g[:], arg[:], SIGMOID)
-                gate.append(g)
-            if b == 0:
-                later_products()
-            term = [keep.tile([P, V], F32, name="term%d_%d" % (b, d)) for d in range(2)]
-            nc.vector.tensor_tensor(term[0][:], hh[:].indirect(pos_sb[0][:]), gate[0][:], MULT)
-
-            z = keep.tile([P, V], F32, name="z%d" % b)
-            pieces = ((0, V),) if b == 0 else ((0, V - TAIL), (V - TAIL, V))
-            for v0, v1 in pieces:
-                nc.vector.tensor_tensor(
-                    term[1][:, v0:v1], hh[:].indirect(pos_sb[1][:, v0 // 16 : v1 // 16]), gate[1][:, v0:v1], MULT
+                nc.tensor.matmul(
+                    turned[:, c * P : (c + 1) * P], term[0][d][:, c * P : (c + 1) * P], ident[:],
+                    is_transpose=True, start=(d == 0), stop=(d == 1),
                 )
-            if b == 0:
-                turned = psum.tile([P, V], F32, name="acc", tag="bank0")
-                for c in range(V // P):
-                    for d in range(2):
-                        nc.tensor.matmul(
-                            turned[:, c * P : (c + 1) * P], term[d][:, c * P : (c + 1) * P], ident[:],
-                            is_transpose=True, start=(d == 0), stop=(d == 1),
-                        )
-                turned_sb = keep.tile([P, V], F32, name="turned_sb")
-                nc.scalar.activation(turned_sb[:], turned[:], COPY)
-                back = psum.tile([P, V], F32, name="acc", tag="bank1")
-                for c in range(V // P):
-                    nc.tensor.transpose(back[:, c * P : (c + 1) * P], turned_sb[:, c * P : (c + 1) * P], ident[:])
-                nc.scalar.activation(z[:], back[:], COPY)
-                nc.sync.dma_start(out[0:P, :], z[:])
-                continue
+        turned_sb = keep.tile([P, V], F32, name="turned_sb")
+        nc.scalar.activation(turned_sb[:], turned[:], COPY)
+        make_gate(1, 1, "term0_0")
+        back = psum.tile([P, V], F32, name="acc", tag="bank1")
+        for c in range(V // P):
+            nc.tensor.transpose(back[:, c * P : (c + 1) * P], turned_sb[:, c * P : (c + 1) * P], ident[:])
+        nc.scalar.activation(z[0][:], back[:], COPY)
+        nc.sync.dma_start(out[0:P, :], z[0][:])
 
-            for v0, v1 in pieces:
-                nc.vector.tensor_tensor(z[:, v0:v1], term[0][:, v0:v1], term[1][:, v0:v1], ADD)
-                (nc.sync if v0 == 0 else nc.scalar).dma_start(out[b * P : (b + 1) * P, v0:v1], z[:, v0:v1])
+        def finish(v0, v1, queue):
+            nc.vector.tensor_tensor(z[1][:, v0:v1], term[1][0][:, v0:v1], term[1][1][:, v0:v1], ADD)
+            queue.dma_start(out[P : 2 * P, v0:v1], z[1][:, v0:v1])
+
+        gated(1, 0, 0, V)
+        gated(1, 1, 0, 256)
+        gated(1, 1, 256, 384)
+        finish(0, 256, nc.sync)
+        gated(1, 1, 384, V)
+        finish(256, 384, nc.scalar)
+        finish(384, V, nc.sync)

@@ -22,7 +22,7 @@ P = 128
 PACK = 4
 HALF = S // 2
 QUARTER = S // 4
-LAST_CHUNKS = ((0, 1792, "scalar"), (1792, 3072, "vector"), (3072, 3840, "vector"), (3840, 4096, "scalar"))
+LAST_CHUNKS = ((0, 1280, "scalar"), (1280, 2304, "scalar"), (2304, 3328, "vector"), (3328, 3712, "scalar"), (3712, 3968, "vector"), (3968, 4096, "scalar"))
 TAIL = 128
 
 
@@ -47,7 +47,9 @@ def tile_picked_gatedg_none_e_kernel(
         nc.vector.memset(warm_in[:], 0.0)
         nc.scalar.activation(warm_out[:], warm_in[:], SIGMOID)
 
-        w_words = [keep.tile([P, N], U32, name="w_words%d" % i, align_bytes=64) for i in range(3)]
+        words12 = keep.tile([P, 2 * N], U32, name="words12", align_bytes=64)
+        words3 = keep.tile([P, N], U32, name="words3", align_bytes=64)
+        w_words = [words12[:, 0:N], words12[:, N : 2 * N], words3[:]]
         scale_tile = keep.tile([P, 2 * N], U8, name="scale_tile", align_bytes=64)
         nc.vector.memset(scale_tile[:].bitcast(I32), 0)
         w_place = ((0, 0), (8, P), (0, N))
@@ -73,7 +75,7 @@ def tile_picked_gatedg_none_e_kernel(
         for c0, c1, eng in LAST_CHUNKS:
             nc.sync.dma_start(plane[3][:, c0:c1], rows[:, 3, c0:c1])
         for i in range(3):
-            nc.sync.dma_start(w_words[i][:].bitcast(I32), words_in[i][0].rearrange("p n t -> p (n t)").bitcast(I32))
+            nc.sync.dma_start(w_words[i].bitcast(I32), words_in[i][0].rearrange("p n t -> p (n t)").bitcast(I32))
         nc.sync.dma_start(cen_sb[:], cen)
         nc.sync.dma_start(pos_sb[0][:], pos1)
         nc.sync.dma_start(pos_sb[1][:], pos2)
@@ -96,16 +98,16 @@ def tile_picked_gatedg_none_e_kernel(
 
         codes = keep.tile([P, S], U32, name="codes", align_bytes=64)
         xsc = keep.tile([P, S], U8, name="xsc", align_bytes=64)
-        acc = psum.tile([P, HALF], F32, name="acc", tag="bank7")
         for n in range(3):
+            acc = psum.tile([P, HALF], F32, name="acc", tag="bank%d" % n)
             nc.tensor.matmul_mx(
-                out=acc[:, 0:N],
+                out=acc[:],
                 lhsT=w_words[0][:, 0:P].bitcast(FP8X4),
                 lhsT_scale=w_scale(0, 0, P),
-                rhs=w_words[0][:].bitcast(FP8X4),
-                rhs_scale=w_scale(0, 0, N),
-                start=(n == 0),
-                stop=(n == 2),
+                rhs=words12[:].bitcast(FP8X4),
+                rhs_scale=scale_tile[:],
+                start=True,
+                stop=True,
             )
 
         res = [[keep.tile([P, S], F32, name="res%d_%d" % (b, i)) for i in range(3)] for b in range(2)]
@@ -145,7 +147,7 @@ def tile_picked_gatedg_none_e_kernel(
         for c0, c1 in ((0, 256), (256, 512), (512, 768), (768, 896), (896, 1024)):
             quantize(c0, c1)
         product(0, 0, (0, 256, 512), 0)
-        product(0, 0, (512, 768), 1)
+        product(0, 0, (512, 768), 1, True)
         product(0, 0, (768, 896), 2, True)
         product(0, 0, (896, 1024), 3)
         low, high = (0, 512), (512, 768, 896, 1024)

@@ -166,14 +166,15 @@ def tile_picked_gatedg_none_e_kernel(
 
         gate = [[None, None], [None, None]]
 
-        def make_gate(b, d, tag):
+        def make_gate(b, d, dst):
             arg = keep.tile([P, V], F32, name="arg%d_%d" % (b, d))
             nc.vector.tensor_tensor(arg[:], res[b][1][:].indirect(pos_sb[d][:]), yc[b][:], ADD)
-            gate[b][d] = keep.tile([P, V], F32, name="gate%d_%d" % (b, d), tag=tag)
-            nc.scalar.activation(gate[b][d][:], arg[:], SIGMOID)
+            gate[b][d] = dst
+            nc.scalar.activation(dst, arg[:], SIGMOID)
 
-        make_gate(0, 0, "gate0_0")
-        make_gate(0, 1, "gate0_1")
+        gates0 = keep.tile([P, 2 * V], F32, name="gates0")
+        make_gate(0, 0, gates0[:, 0:V])
+        make_gate(0, 1, gates0[:, V : 2 * V])
         product(1, 1, low, 4)
         product(1, 1, high, 5)
         product(1, 2, low, 6)
@@ -187,23 +188,28 @@ def tile_picked_gatedg_none_e_kernel(
                 term[b][d][:, v0:v1], res[b][2][:].indirect(pos_sb[d][:, v0 // 16 : v1 // 16]), gate[b][d][:, v0:v1], MULT
             )
 
-        gated(0, 0, 0, V)
-        gated(0, 1, 0, V)
-        make_gate(1, 0, "gate1_0")
-        turned = psum.tile([P, V], F32, name="acc", tag="bank0")
-        for c in range(V // P):
-            for d in range(2):
-                nc.tensor.matmul(
-                    turned[:, c * P : (c + 1) * P], term[0][d][:, c * P : (c + 1) * P], ident[:],
-                    is_transpose=True, start=(d == 0), stop=(d == 1),
-                )
-        turned_sb = keep.tile([P, V], F32, name="turned_sb")
-        nc.scalar.activation(turned_sb[:], turned[:], COPY)
-        make_gate(1, 1, "term0_0")
-        back = psum.tile([P, V], F32, name="acc", tag="bank1")
-        for c in range(V // P):
-            nc.tensor.transpose(back[:, c * P : (c + 1) * P], turned_sb[:, c * P : (c + 1) * P], ident[:])
-        nc.scalar.activation(z[0][:], back[:], COPY)
+        blocks = [slice(c * P, (c + 1) * P) for c in range(V // P)]
+        turned = [psum.tile([P, HALF], F32, name="acc", tag="bank%d" % c) for c in range(V // P)]
+        turned_sb = keep.tile([P, V], F32, name="turned_sb", tag="turned_sb")
+        for d in range(2):
+            gated(0, d, 0, V)
+            for c, cols in enumerate(blocks):
+                nc.tensor.matmul(turned[c][:, 0:P], term[0][d][:, cols], ident[:], is_transpose=True, start=(d == 0), stop=(d == 1))
+        gates1 = keep.tile([P, 2 * V], F32, name="gates1", tag="term0_1")
+        for c, cols in enumerate(blocks):
+            nc.scalar.activation(turned_sb[:, cols], turned[c][:, 0:P], COPY)
+            if c % 2 == 1:
+                make_gate(1, c // 2, gates1[:, (c // 2) * V : (c // 2 + 1) * V])
+        back = [psum.tile([P, HALF], F32, name="acc", tag="bank%d" % (4 + u)) for u in range(2)]
+        for c, cols in enumerate(blocks):
+            nc.tensor.transpose(back[c // 2][:, (c % 2) * P : (c % 2 + 1) * P], turned_sb[:, cols], ident[:])
+
+        def store_sum(u):
+            cols = slice(u * 2 * P, (u + 1) * 2 * P)
+            nc.scalar.activation(z[0][:, cols], back[u][:, 0 : 2 * P], COPY)
+
+        store_sum(0)
+        store_sum(1)
         nc.sync.dma_start(out[0:P, :], z[0][:])
 
         def finish(v0, v1, queue):

@@ -166,15 +166,14 @@ def tile_picked_gatedg_none_e_kernel(
 
         gate = [[None, None], [None, None]]
 
-        def make_gate(b, d, dst):
+        def make_gate(b, d, tag):
             arg = keep.tile([P, V], F32, name="arg%d_%d" % (b, d))
             nc.vector.tensor_tensor(arg[:], res[b][1][:].indirect(pos_sb[d][:]), yc[b][:], ADD)
-            gate[b][d] = dst
-            nc.scalar.activation(dst, arg[:], SIGMOID)
+            gate[b][d] = keep.tile([P, V], F32, name="gate%d_%d" % (b, d), tag=tag)
+            nc.scalar.activation(gate[b][d][:], arg[:], SIGMOID)
 
-        gates0 = keep.tile([P, 2 * V], F32, name="gates0")
-        make_gate(0, 0, gates0[:, 0:V])
-        make_gate(0, 1, gates0[:, V : 2 * V])
+        make_gate(0, 0, "gate0_0")
+        make_gate(0, 1, "gate0_1")
         product(1, 1, low, 4)
         product(1, 1, high, 5)
         product(1, 2, low, 6)
@@ -195,11 +194,9 @@ def tile_picked_gatedg_none_e_kernel(
             gated(0, d, 0, V)
             for c, cols in enumerate(blocks):
                 nc.tensor.matmul(turned[c][:, 0:P], term[0][d][:, cols], ident[:], is_transpose=True, start=(d == 0), stop=(d == 1))
-        gates1 = keep.tile([P, 2 * V], F32, name="gates1", tag="term0_1")
         for c, cols in enumerate(blocks):
             nc.scalar.activation(turned_sb[:, cols], turned[c][:, 0:P], COPY)
-            if c % 2 == 1:
-                make_gate(1, c // 2, gates1[:, (c // 2) * V : (c // 2 + 1) * V])
+        make_gate(1, 0, "term0_1")
         back = [psum.tile([P, HALF], F32, name="acc", tag="bank%d" % (4 + u)) for u in range(2)]
         for c, cols in enumerate(blocks):
             nc.tensor.transpose(back[c // 2][:, (c % 2) * P : (c % 2 + 1) * P], turned_sb[:, cols], ident[:])
@@ -211,15 +208,14 @@ def tile_picked_gatedg_none_e_kernel(
         store_sum(0)
         store_sum(1)
         nc.sync.dma_start(out[0:P, :], z[0][:])
+        make_gate(1, 1, "turned_sb")
 
         def finish(v0, v1, queue):
             nc.vector.tensor_tensor(z[1][:, v0:v1], term[1][0][:, v0:v1], term[1][1][:, v0:v1], ADD)
             queue.dma_start(out[P : 2 * P, v0:v1], z[1][:, v0:v1])
 
         gated(1, 0, 0, V)
-        gated(1, 1, 0, 256)
-        gated(1, 1, 256, 384)
-        finish(0, 256, nc.sync)
-        gated(1, 1, 384, V)
-        finish(256, 384, nc.scalar)
-        finish(384, V, nc.sync)
+        gated(1, 1, 0, V // 2)
+        gated(1, 1, V // 2, V)
+        finish(0, V // 2, nc.sync)
+        finish(V // 2, V, nc.scalar)

@@ -20,10 +20,23 @@ SIGMOID = mybir.ActivationFunctionType.Sigmoid
 
 P = 128
 PACK = 4
+LIST_ROWS = 16
+BANK = 512
 HALF = S // 2
-QUARTER = S // 4
-LAST_CHUNKS = ((0, 1280, "scalar"), (1280, 2304, "scalar"), (2304, 3328, "vector"), (3328, 3712, "scalar"), (3712, 3968, "vector"), (3968, 4096, "scalar"))
-TAIL = 128
+Y, E, H = 0, 1, 2
+
+LAST_CHUNKS = (
+    (0, 1280, "scalar"),
+    (1280, 2304, "scalar"),
+    (2304, 3328, "vector"),
+    (3328, 3712, "scalar"),
+    (3712, 3968, "vector"),
+    (3968, 4096, "scalar"),
+)
+CUTS = (0, 256, 512, 768, 896, 1024)
+LAST_PIECE = CUTS[-2]
+W_SCALE_AT = ((0, 0), (8, P), (0, N))
+LAST_SCALE_AT = (4, P)
 
 
 def tile_picked_gatedg_none_e_kernel(
@@ -34,9 +47,12 @@ def tile_picked_gatedg_none_e_kernel(
         keep = ctx.enter_context(tc.tile_pool(name="keep", bufs=1))
         psum = ctx.enter_context(tc.psum_pool(name="psum", bufs=1))
 
-        offs_sb = keep.tile([P, S // 16], U16, name="offs_sb")
-        cen_sb = keep.tile([P, V // 16], U16, name="cen_sb")
-        pos_sb = [keep.tile([P, V // 16], U16, name="pos%d_sb" % d) for d in range(2)]
+        def bank_tile(bank):
+            return psum.tile([P, BANK], F32, name="acc", tag="bank%d" % bank)
+
+        offs_sb = keep.tile([P, S // LIST_ROWS], U16, name="offs_sb")
+        cen_sb = keep.tile([P, V // LIST_ROWS], U16, name="cen_sb")
+        pos_sb = [keep.tile([P, V // LIST_ROWS], U16, name="pos%d_sb" % d) for d in range(2)]
 
         rows = xT.rearrange("(p j) t -> p j t", j=PACK)
         plane = [keep.tile([P, T], F32, name="plane%d" % j) for j in range(PACK)]
@@ -47,34 +63,35 @@ def tile_picked_gatedg_none_e_kernel(
         nc.vector.memset(warm_in[:], 0.0)
         nc.scalar.activation(warm_out[:], warm_in[:], SIGMOID)
 
-        words12 = keep.tile([P, 2 * N], U32, name="words12", align_bytes=64)
-        words3 = keep.tile([P, N], U32, name="words3", align_bytes=64)
-        w_words = [words12[:, 0:N], words12[:, N : 2 * N], words3[:]]
+        w_tiles = [keep.tile([P, N], U32, name="w_words%d" % i, align_bytes=64) for i in (Y, E, H)]
+        w_words = [tile[:] for tile in w_tiles]
         scale_tile = keep.tile([P, 2 * N], U8, name="scale_tile", align_bytes=64)
         nc.vector.memset(scale_tile[:].bitcast(I32), 0)
-        w_place = ((0, 0), (8, P), (0, N))
         words_in = (w1_words, w2_words, w3_words)
         scales_in = (w1_scales, w2_scales, w3_scales)
 
         def w_scale(i, c0, c1):
-            r, c = w_place[i]
-            return scale_tile[r:P, c + c0 : c + c1]
+            row, col = W_SCALE_AT[i]
+            return scale_tile[row:P, col + c0 : col + c1]
 
         def load_scales(queue, i):
-            r, c = w_place[i]
+            row, col = W_SCALE_AT[i]
             for q in range(4):
-                queue.dma_start(scale_tile[32 * q + r : 32 * q + r + 4, c : c + N].bitcast(I32), scales_in[i][0, 4 * q : 4 * q + 4, :].bitcast(I32))
+                queue.dma_start(
+                    scale_tile[32 * q + row : 32 * q + row + 4, col : col + N].bitcast(I32),
+                    scales_in[i][0, 4 * q : 4 * q + 4, :].bitcast(I32),
+                )
 
         nc.sync.dma_start(plane[0][:], rows[:, 0, :])
         nc.sync.dma_start(offs_sb[:], offs)
         nc.sync.dma_start(plane[1][:], rows[:, 1, :])
-        load_scales(nc.gpsimd, 0)
-        load_scales(nc.gpsimd, 1)
-        load_scales(nc.sync, 2)
+        load_scales(nc.gpsimd, Y)
+        load_scales(nc.gpsimd, E)
+        load_scales(nc.sync, H)
         nc.sync.dma_start(plane[2][:], rows[:, 2, :])
-        for c0, c1, eng in LAST_CHUNKS:
+        for c0, c1, engine in LAST_CHUNKS:
             nc.sync.dma_start(plane[3][:, c0:c1], rows[:, 3, c0:c1])
-        for i in range(3):
+        for i in (Y, E, H):
             nc.sync.dma_start(w_words[i].bitcast(I32), words_in[i][0].rearrange("p n t -> p (n t)").bitcast(I32))
         nc.sync.dma_start(cen_sb[:], cen)
         nc.sync.dma_start(pos_sb[0][:], pos1)
@@ -83,58 +100,48 @@ def tile_picked_gatedg_none_e_kernel(
         ident = keep.tile([P, P], F32, name="ident")
         make_identity(nc, ident[:])
 
-        picked = [keep.tile([P, HALF, PACK], BF16, name="picked%d" % h, align_bytes=64) for h in range(2)]
-        lists = [offs_sb[:, h * (HALF // 16) : (h + 1) * (HALF // 16)] for h in range(2)]
+        picked = [keep.tile([P, HALF, PACK], BF16, name="picked%d" % u, align_bytes=64) for u in range(2)]
+        offs_half = [offs_sb[:, u * (HALF // LIST_ROWS) : (u + 1) * (HALF // LIST_ROWS)] for u in range(2)]
         for j in range(PACK - 1):
-            for h in range(2):
-                nc.vector.tensor_copy(picked[h][:, :, j], plane[j][:].indirect(lists[h]))
-        for c0, c1, eng in LAST_CHUNKS:
-            if eng == "scalar":
+            for u in range(2):
+                nc.vector.tensor_copy(picked[u][:, :, j], plane[j][:].indirect(offs_half[u]))
+        for c0, c1, engine in LAST_CHUNKS:
+            if engine == "scalar":
                 nc.scalar.activation(last_bf[:, c0:c1], plane[3][:, c0:c1], COPY)
             else:
                 nc.vector.tensor_copy(last_bf[:, c0:c1], plane[3][:, c0:c1])
-        nc.vector.tensor_copy(picked[0][:, :, 3], plane[3][:].indirect(lists[0]))
-        nc.scalar.activation(picked[1][:, :, 3], last_bf[:].indirect(lists[1]), COPY)
+        nc.vector.tensor_copy(picked[0][:, :, 3], plane[3][:].indirect(offs_half[0]))
+        nc.scalar.activation(picked[1][:, :, 3], last_bf[:].indirect(offs_half[1]), COPY)
 
         codes = keep.tile([P, S], U32, name="codes", align_bytes=64)
-        xsc = keep.tile([P, S], U8, name="xsc", align_bytes=64)
-        for n in range(3):
-            acc = psum.tile([P, HALF], F32, name="acc", tag="bank%d" % n)
-            nc.tensor.matmul_mx(
-                out=acc[:],
-                lhsT=w_words[0][:, 0:P].bitcast(FP8X4),
-                lhsT_scale=w_scale(0, 0, P),
-                rhs=words12[:].bitcast(FP8X4),
-                rhs_scale=scale_tile[:],
-                start=True,
-                stop=True,
-            )
+        x_scale_tile = keep.tile([P, S], U8, name="x_scale_tile", align_bytes=64)
 
-        res = [[keep.tile([P, S], F32, name="res%d_%d" % (b, i)) for i in range(3)] for b in range(2)]
+        res = [[keep.tile([P, S], F32, name="res%d_%d" % (b, i)) for i in (Y, E, H)] for b in range(2)]
 
-        def x_scales(c0, c1):
-            if c0 >= S - P:
-                return scale_tile[4:P, P + c0 - (S - P) : P + c1 - (S - P)]
-            return xsc[:, c0:c1]
+        def x_scale(c0, c1):
+            if c0 >= LAST_PIECE:
+                row, col = LAST_SCALE_AT
+                return scale_tile[row:P, col + c0 - LAST_PIECE : col + c1 - LAST_PIECE]
+            return x_scale_tile[:, c0:c1]
 
-        def quantize(c0, c1):
-            h = c0 // HALF
+        for c0, c1 in zip(CUTS[:-1], CUTS[1:]):
+            u = c0 // HALF
             nc.vector.quantize_mx(
                 out=codes[:, c0:c1].bitcast(FP8X4),
-                scales=x_scales(c0, c1),
-                in_=picked[h][:, c0 - h * HALF : c1 - h * HALF, :].rearrange("p n j -> p (n j)"),
+                scales=x_scale(c0, c1),
+                in_=picked[u][:, c0 - u * HALF : c1 - u * HALF, :].rearrange("p n j -> p (n j)"),
             )
 
         def product(b, i, cuts, bank, on_vector=False):
             c0, c1 = cuts[0], cuts[-1]
-            acc = psum.tile([P, HALF], F32, name="acc", tag="bank%d" % bank)
+            acc = bank_tile(bank)
             for a0, a1 in zip(cuts[:-1], cuts[1:]):
                 nc.tensor.matmul_mx(
                     out=acc[:, a0 - c0 : a1 - c0],
                     lhsT=w_words[i][:, b * P : (b + 1) * P].bitcast(FP8X4),
                     lhsT_scale=w_scale(i, b * P, (b + 1) * P),
                     rhs=codes[:, a0:a1].bitcast(FP8X4),
-                    rhs_scale=x_scales(a0, a1),
+                    rhs_scale=x_scale(a0, a1),
                     start=True,
                     stop=True,
                 )
@@ -144,78 +151,73 @@ def tile_picked_gatedg_none_e_kernel(
             else:
                 nc.scalar.activation(dst, acc[:, 0 : c1 - c0], COPY)
 
-        for c0, c1 in ((0, 256), (256, 512), (512, 768), (768, 896), (896, 1024)):
-            quantize(c0, c1)
-        product(0, 0, (0, 256, 512), 0)
-        product(0, 0, (512, 768), 1, True)
-        product(0, 0, (768, 896), 2, True)
-        product(0, 0, (896, 1024), 3)
-        low, high = (0, 512), (512, 768, 896, 1024)
-        product(1, 0, (0, 256), 4)
-        product(1, 0, (256, 512), 5)
-        product(1, 0, (512, 768), 6)
-        product(1, 0, (768, 896, 1024), 7)
-        product(0, 1, low, 0)
-        product(0, 1, high, 1)
-        product(0, 2, low, 2)
-        product(0, 2, high, 3)
+        def product_in_halves(b, i, bank):
+            product(b, i, (0, HALF), bank)
+            product(b, i, CUTS[2:], bank + 1)
 
-        yc = [keep.tile([P, V], F32, name="yc%d" % b) for b in range(2)]
+        product(0, Y, CUTS[0:3], 0)
+        product(0, Y, CUTS[2:4], 1, on_vector=True)
+        product(0, Y, CUTS[3:5], 2, on_vector=True)
+        product(0, Y, CUTS[4:6], 3)
+        product(1, Y, CUTS[0:2], 4)
+        product(1, Y, CUTS[1:3], 5)
+        product(1, Y, CUTS[2:4], 6)
+        product(1, Y, CUTS[3:6], 7)
+        product_in_halves(0, E, 0)
+        product_in_halves(0, H, 2)
+
+        centre = [keep.tile([P, V], F32, name="centre%d" % b) for b in range(2)]
         for b in range(2):
-            nc.vector.tensor_copy(yc[b][:], res[b][0][:].indirect(cen_sb[:]))
+            nc.vector.tensor_copy(centre[b][:], res[b][Y][:].indirect(cen_sb[:]))
 
-        gate = [[None, None], [None, None]]
+        gate = {}
 
-        def make_gate(b, d, tag):
+        def make_gate(b, d, slot):
             arg = keep.tile([P, V], F32, name="arg%d_%d" % (b, d))
-            nc.vector.tensor_tensor(arg[:], res[b][1][:].indirect(pos_sb[d][:]), yc[b][:], ADD)
-            gate[b][d] = keep.tile([P, V], F32, name="gate%d_%d" % (b, d), tag=tag)
-            nc.scalar.activation(gate[b][d][:], arg[:], SIGMOID)
+            nc.vector.tensor_tensor(arg[:], res[b][E][:].indirect(pos_sb[d][:]), centre[b][:], ADD)
+            gate[b, d] = keep.tile([P, V], F32, name="gate%d_%d" % (b, d), tag=slot)
+            nc.scalar.activation(gate[b, d][:], arg[:], SIGMOID)
 
         make_gate(0, 0, "gate0_0")
         make_gate(0, 1, "gate0_1")
-        product(1, 1, low, 4)
-        product(1, 1, high, 5)
-        product(1, 2, low, 6)
-        product(1, 2, high, 7)
+        product_in_halves(1, E, 4)
+        product_in_halves(1, H, 6)
 
         term = [[keep.tile([P, V], F32, name="term%d_%d" % (b, d), tag="term%d_%d" % (b, d)) for d in range(2)] for b in range(2)]
         z = [keep.tile([P, V], F32, name="z%d" % b) for b in range(2)]
 
         def gated(b, d, v0, v1):
             nc.vector.tensor_tensor(
-                term[b][d][:, v0:v1], res[b][2][:].indirect(pos_sb[d][:, v0 // 16 : v1 // 16]), gate[b][d][:, v0:v1], MULT
+                term[b][d][:, v0:v1],
+                res[b][H][:].indirect(pos_sb[d][:, v0 // LIST_ROWS : v1 // LIST_ROWS]),
+                gate[b, d][:, v0:v1],
+                MULT,
             )
 
-        blocks = [slice(c * P, (c + 1) * P) for c in range(V // P)]
-        turned = [psum.tile([P, HALF], F32, name="acc", tag="bank%d" % c) for c in range(V // P)]
+        squares = [slice(c * P, (c + 1) * P) for c in range(V // P)]
+        turned = [bank_tile(c) for c in range(len(squares))]
         turned_sb = keep.tile([P, V], F32, name="turned_sb", tag="turned_sb")
         for d in range(2):
             gated(0, d, 0, V)
-            for c, cols in enumerate(blocks):
-                nc.tensor.matmul(turned[c][:, 0:P], term[0][d][:, cols], ident[:], is_transpose=True, start=(d == 0), stop=(d == 1))
-        for c, cols in enumerate(blocks):
+            for c, cols in enumerate(squares):
+                nc.tensor.matmul(
+                    turned[c][:, 0:P], term[0][d][:, cols], ident[:], is_transpose=True, start=(d == 0), stop=(d == 1)
+                )
+        for c, cols in enumerate(squares):
             nc.scalar.activation(turned_sb[:, cols], turned[c][:, 0:P], COPY)
         make_gate(1, 0, "term0_1")
-        back = [psum.tile([P, HALF], F32, name="acc", tag="bank%d" % (4 + u)) for u in range(2)]
-        for c, cols in enumerate(blocks):
+        back = [bank_tile(len(squares) + u) for u in range(2)]
+        for c, cols in enumerate(squares):
             nc.tensor.transpose(back[c // 2][:, (c % 2) * P : (c % 2 + 1) * P], turned_sb[:, cols], ident[:])
-
-        def store_sum(u):
-            cols = slice(u * 2 * P, (u + 1) * 2 * P)
-            nc.scalar.activation(z[0][:, cols], back[u][:, 0 : 2 * P], COPY)
-
-        store_sum(0)
-        store_sum(1)
+        halves = ((0, V // 2), (V // 2, V))
+        for u, (v0, v1) in enumerate(halves):
+            nc.scalar.activation(z[0][:, v0:v1], back[u][:, 0 : v1 - v0], COPY)
         nc.sync.dma_start(out[0:P, :], z[0][:])
         make_gate(1, 1, "turned_sb")
 
-        def finish(v0, v1, queue):
-            nc.vector.tensor_tensor(z[1][:, v0:v1], term[1][0][:, v0:v1], term[1][1][:, v0:v1], ADD)
-            queue.dma_start(out[P : 2 * P, v0:v1], z[1][:, v0:v1])
-
         gated(1, 0, 0, V)
-        gated(1, 1, 0, V // 2)
-        gated(1, 1, V // 2, V)
-        finish(0, V // 2, nc.sync)
-        finish(V // 2, V, nc.scalar)
+        for v0, v1 in halves:
+            gated(1, 1, v0, v1)
+        for v0, v1 in halves:
+            nc.vector.tensor_tensor(z[1][:, v0:v1], term[1][0][:, v0:v1], term[1][1][:, v0:v1], ADD)
+        nc.scalar.dma_start(out[P : 2 * P, :], z[1][:])

@@ -74,21 +74,22 @@ def tile_picked_gatedg_none_e_kernel(
             row, col = W_SCALE_AT[i]
             return scale_tile[row:P, col + c0 : col + c1]
 
-        def load_scales(queue, i):
-            row, col = W_SCALE_AT[i]
-            for q in range(4):
-                queue.dma_start(
+        def load_scales(first, last):
+            for n in range(first, last):
+                i, q = divmod(n, 4)
+                row, col = W_SCALE_AT[i]
+                nc.sync.dma_start(
                     scale_tile[32 * q + row : 32 * q + row + 4, col : col + N].bitcast(I32),
                     scales_in[i][0, 4 * q : 4 * q + 4, :].bitcast(I32),
                 )
 
         nc.sync.dma_start(plane[0][:], rows[:, 0, :])
         nc.sync.dma_start(offs_sb[:], offs)
+        load_scales(0, 5)
         nc.sync.dma_start(plane[1][:], rows[:, 1, :])
-        load_scales(nc.gpsimd, Y)
-        load_scales(nc.gpsimd, E)
-        load_scales(nc.sync, H)
+        load_scales(5, 11)
         nc.sync.dma_start(plane[2][:], rows[:, 2, :])
+        load_scales(11, 12)
         for c0, c1, engine in LAST_CHUNKS:
             nc.sync.dma_start(plane[3][:, c0:c1], rows[:, 3, c0:c1])
         for i in (Y, E, H):
@@ -159,27 +160,35 @@ def tile_picked_gatedg_none_e_kernel(
         product(0, Y, CUTS[2:4], 1, on_vector=True)
         product(0, Y, CUTS[3:5], 2, on_vector=True)
         product(0, Y, CUTS[4:6], 3)
-        product(1, Y, CUTS[0:2], 4)
-        product(1, Y, CUTS[1:3], 5)
-        product(1, Y, CUTS[2:4], 6)
-        product(1, Y, CUTS[3:6], 7)
-        product_in_halves(0, E, 0)
+        product(0, E, CUTS[0:2], 4)
+        product(0, E, CUTS[1:3], 5)
+        product(0, E, CUTS[2:4], 6)
+        product(0, E, CUTS[3:6], 7)
+        product_in_halves(1, Y, 0)
         product_in_halves(0, H, 2)
+        halves = ((0, V // 2), (V // 2, V))
 
         centre = [keep.tile([P, V], F32, name="centre%d" % b) for b in range(2)]
-        for b in range(2):
-            nc.vector.tensor_copy(centre[b][:], res[b][Y][:].indirect(cen_sb[:]))
+        for v0, v1 in halves:
+            nc.vector.tensor_copy(centre[0][:, v0:v1], res[0][Y][:].indirect(cen_sb[:, v0 // LIST_ROWS : v1 // LIST_ROWS]))
 
         gate = {}
 
-        def make_gate(b, d, slot):
+        def make_gate(b, d, slot, spans=((0, V),)):
             arg = keep.tile([P, V], F32, name="arg%d_%d" % (b, d))
-            nc.vector.tensor_tensor(arg[:], res[b][E][:].indirect(pos_sb[d][:]), centre[b][:], ADD)
+            for v0, v1 in spans:
+                nc.vector.tensor_tensor(
+                    arg[:, v0:v1],
+                    res[b][E][:].indirect(pos_sb[d][:, v0 // LIST_ROWS : v1 // LIST_ROWS]),
+                    centre[b][:, v0:v1],
+                    ADD,
+                )
             gate[b, d] = keep.tile([P, V], F32, name="gate%d_%d" % (b, d), tag=slot)
             nc.scalar.activation(gate[b, d][:], arg[:], SIGMOID)
 
-        make_gate(0, 0, "gate0_0")
+        make_gate(0, 0, "gate0_0", halves)
         make_gate(0, 1, "gate0_1")
+        nc.vector.tensor_copy(centre[1][:], res[1][Y][:].indirect(cen_sb[:]))
         product_in_halves(1, E, 4)
         product_in_halves(1, H, 6)
 
@@ -209,7 +218,6 @@ def tile_picked_gatedg_none_e_kernel(
         back = [bank_tile(len(squares) + u) for u in range(2)]
         for c, cols in enumerate(squares):
             nc.tensor.transpose(back[c // 2][:, (c % 2) * P : (c % 2 + 1) * P], turned_sb[:, cols], ident[:])
-        halves = ((0, V // 2), (V // 2, V))
         for u, (v0, v1) in enumerate(halves):
             nc.scalar.activation(z[0][:, v0:v1], back[u][:, 0 : v1 - v0], COPY)
         nc.sync.dma_start(out[0:P, :], z[0][:])
@@ -220,4 +228,5 @@ def tile_picked_gatedg_none_e_kernel(
             gated(1, 1, v0, v1)
         for v0, v1 in halves:
             nc.vector.tensor_tensor(z[1][:, v0:v1], term[1][0][:, v0:v1], term[1][1][:, v0:v1], ADD)
-        nc.scalar.dma_start(out[P : 2 * P, :], z[1][:])
+        for queue, (v0, v1) in zip((nc.sync, nc.scalar), halves):
+            queue.dma_start(out[P : 2 * P, v0:v1], z[1][:, v0:v1])

@@ -1,7 +1,6 @@
 from contextlib import ExitStack
 
 import concourse.mybir as mybir
-from concourse.masks import make_identity
 
 K, T, S, V, N = 512, 4096, 1024, 512, 256
 FLOPS = 3 * 2 * K * N * S
@@ -35,7 +34,7 @@ LAST_CHUNKS = (
 )
 CUTS = (0, 256, 512, 768, 896, 1024)
 LAST_PIECE = CUTS[-2]
-W_SCALE_AT = ((0, 0), (8, P), (0, N))
+W_SCALE_AT = ((0, 0), (8, 0), (0, N))
 LAST_SCALE_AT = (4, P)
 
 
@@ -98,9 +97,6 @@ def tile_picked_gatedg_none_e_kernel(
         nc.sync.dma_start(pos_sb[0][:], pos1)
         nc.sync.dma_start(pos_sb[1][:], pos2)
 
-        ident = keep.tile([P, P], F32, name="ident")
-        make_identity(nc, ident[:])
-
         picked = [keep.tile([P, HALF, PACK], BF16, name="picked%d" % u, align_bytes=64) for u in range(2)]
         offs_half = [offs_sb[:, u * (HALF // LIST_ROWS) : (u + 1) * (HALF // LIST_ROWS)] for u in range(2)]
         for j in range(PACK - 1):
@@ -156,77 +152,74 @@ def tile_picked_gatedg_none_e_kernel(
             product(b, i, (0, HALF), bank)
             product(b, i, CUTS[2:], bank + 1)
 
-        product(0, Y, CUTS[0:3], 0)
-        product(0, Y, CUTS[2:4], 1, on_vector=True)
-        product(0, Y, CUTS[3:5], 2, on_vector=True)
-        product(0, Y, CUTS[4:6], 3)
-        product(0, E, CUTS[0:2], 4)
-        product(0, E, CUTS[1:3], 5)
-        product(0, E, CUTS[2:4], 6)
-        product(0, E, CUTS[3:6], 7)
-        product_in_halves(1, Y, 0)
-        product_in_halves(0, H, 2)
+        product(0, Y, CUTS[0:2], 0)
+        product(0, E, CUTS[0:2], 1)
+        product(0, Y, CUTS[1:3], 2)
+        product(0, E, CUTS[1:3], 3)
+        product(0, Y, CUTS[2:4], 4, on_vector=True)
+        product(0, Y, CUTS[3:5], 5, on_vector=True)
+        product(0, Y, CUTS[4:6], 6)
+        product(0, E, CUTS[2:4], 7)
+        product(0, E, CUTS[3:6], 0)
         halves = ((0, V // 2), (V // 2, V))
 
+        def offsets(list_sb, v0, v1):
+            return list_sb[:, v0 // LIST_ROWS : v1 // LIST_ROWS]
+
         centre = [keep.tile([P, V], F32, name="centre%d" % b) for b in range(2)]
-        for v0, v1 in halves:
-            nc.vector.tensor_copy(centre[0][:, v0:v1], res[0][Y][:].indirect(cen_sb[:, v0 // LIST_ROWS : v1 // LIST_ROWS]))
-
-        gate = {}
-
-        def make_gate(b, d, slot, spans=((0, V),)):
-            arg = keep.tile([P, V], F32, name="arg%d_%d" % (b, d))
-            for v0, v1 in spans:
-                nc.vector.tensor_tensor(
-                    arg[:, v0:v1],
-                    res[b][E][:].indirect(pos_sb[d][:, v0 // LIST_ROWS : v1 // LIST_ROWS]),
-                    centre[b][:, v0:v1],
-                    ADD,
-                )
-            gate[b, d] = keep.tile([P, V], F32, name="gate%d_%d" % (b, d), tag=slot)
-            nc.scalar.activation(gate[b, d][:], arg[:], SIGMOID)
-
-        make_gate(0, 0, "gate0_0", halves)
-        make_gate(0, 1, "gate0_1")
-        nc.vector.tensor_copy(centre[1][:], res[1][Y][:].indirect(cen_sb[:]))
-        product_in_halves(1, E, 4)
-        product_in_halves(1, H, 6)
-
-        term = [[keep.tile([P, V], F32, name="term%d_%d" % (b, d), tag="term%d_%d" % (b, d)) for d in range(2)] for b in range(2)]
+        arg = [[keep.tile([P, V], F32, name="arg%d_%d" % (b, d)) for d in range(2)] for b in range(2)]
+        gate = [[keep.tile([P, V], F32, name="gate%d_%d" % (b, d)) for d in range(2)] for b in range(2)]
+        term = [[keep.tile([P, V], F32, name="term%d_%d" % (b, d)) for d in range(2)] for b in range(2)]
         z = [keep.tile([P, V], F32, name="z%d" % b) for b in range(2)]
+        passed = keep.tile([P, V // 2], F32, name="passed")
 
-        def gated(b, d, v0, v1):
+        def gate_arg(b, d, v0=0, v1=V):
             nc.vector.tensor_tensor(
-                term[b][d][:, v0:v1],
-                res[b][H][:].indirect(pos_sb[d][:, v0 // LIST_ROWS : v1 // LIST_ROWS]),
-                gate[b, d][:, v0:v1],
-                MULT,
+                arg[b][d][:, v0:v1], res[b][E][:].indirect(offsets(pos_sb[d], v0, v1)), centre[b][:, v0:v1], ADD
             )
 
-        squares = [slice(c * P, (c + 1) * P) for c in range(V // P)]
-        turned = [bank_tile(c) for c in range(len(squares))]
-        turned_sb = keep.tile([P, V], F32, name="turned_sb", tag="turned_sb")
-        for d in range(2):
-            gated(0, d, 0, V)
-            for c, cols in enumerate(squares):
-                nc.tensor.matmul(
-                    turned[c][:, 0:P], term[0][d][:, cols], ident[:], is_transpose=True, start=(d == 0), stop=(d == 1)
-                )
-        for c, cols in enumerate(squares):
-            nc.scalar.activation(turned_sb[:, cols], turned[c][:, 0:P], COPY)
-        make_gate(1, 0, "term0_1")
-        back = [bank_tile(len(squares) + u) for u in range(2)]
-        for c, cols in enumerate(squares):
-            nc.tensor.transpose(back[c // 2][:, (c % 2) * P : (c % 2 + 1) * P], turned_sb[:, cols], ident[:])
-        for u, (v0, v1) in enumerate(halves):
-            nc.scalar.activation(z[0][:, v0:v1], back[u][:, 0 : v1 - v0], COPY)
-        nc.sync.dma_start(out[0:P, :], z[0][:])
-        make_gate(1, 1, "turned_sb")
+        def squash(b, d):
+            nc.scalar.activation(gate[b][d][:], arg[b][d][:], SIGMOID)
 
-        gated(1, 0, 0, V)
+        def gated(b, d, v0=0, v1=V):
+            nc.vector.tensor_tensor(
+                term[b][d][:, v0:v1], res[b][H][:].indirect(offsets(pos_sb[d], v0, v1)), gate[b][d][:, v0:v1], MULT
+            )
+
         for v0, v1 in halves:
-            gated(1, 1, v0, v1)
+            nc.vector.tensor_copy(centre[0][:, v0:v1], res[0][Y][:].indirect(offsets(cen_sb, v0, v1)))
+        product_in_halves(0, H, 5)
         for v0, v1 in halves:
+            gate_arg(0, 0, v0, v1)
+        product(1, Y, (0, HALF), 1)
+        product(1, Y, CUTS[2:], 2)
+        squash(0, 0)
+        product(1, E, (0, HALF), 3)
+        gate_arg(0, 1)
+        squash(0, 1)
+        nc.scalar.activation(centre[1][:], res[1][Y][:].indirect(cen_sb[:]), COPY)
+        product(1, E, CUTS[2:], 4)
+        gated(0, 0)
+        for v0, v1 in halves:
+            gated(0, 1, v0, v1)
+        for v0, v1 in halves:
+            nc.vector.tensor_tensor(z[0][:, v0:v1], term[0][0][:, v0:v1], term[0][1][:, v0:v1], ADD)
+        nc.sync.dma_start(out[0:P, :], z[0][:])
+        product(1, H, (0, HALF), 7)
+        product(1, H, CUTS[2:], 0)
+
+        def fetch_passed(v0, v1):
+            nc.scalar.activation(passed[:, v0:v1], res[1][H][:].indirect(offsets(pos_sb[1], v0, v1)), COPY)
+
+        gate_arg(1, 0)
+        squash(1, 0)
+        fetch_passed(*halves[0])
+        gate_arg(1, 1)
+        squash(1, 1)
+        gated(1, 0)
+        gated(1, 1, *halves[1])
+        v0, v1 = halves[0]
+        nc.vector.tensor_tensor(term[1][1][:, v0:v1], passed[:, v0:v1], gate[1][1][:, v0:v1], MULT)
+        for queue, (v0, v1) in zip((nc.sync, nc.scalar), reversed(halves)):
             nc.vector.tensor_tensor(z[1][:, v0:v1], term[1][0][:, v0:v1], term[1][1][:, v0:v1], ADD)
-        for queue, (v0, v1) in zip((nc.sync, nc.scalar), halves):
             queue.dma_start(out[P : 2 * P, v0:v1], z[1][:, v0:v1])

@@ -159,7 +159,7 @@ def tile_picked_gatedg_none_e_kernel(
         product(0, Y, CUTS[2:4], 4, on_vector=True)
         product(0, Y, CUTS[3:5], 5, on_vector=True)
         product(0, Y, CUTS[4:6], 6)
-        product(0, E, CUTS[2:4], 7)
+        product(0, E, CUTS[2:4], 7, on_vector=True)
         product(0, E, CUTS[3:6], 0)
         halves = ((0, V // 2), (V // 2, V))
 
@@ -171,55 +171,61 @@ def tile_picked_gatedg_none_e_kernel(
         gate = [[keep.tile([P, V], F32, name="gate%d_%d" % (b, d)) for d in range(2)] for b in range(2)]
         term = [[keep.tile([P, V], F32, name="term%d_%d" % (b, d)) for d in range(2)] for b in range(2)]
         z = [keep.tile([P, V], F32, name="z%d" % b) for b in range(2)]
-        passed = keep.tile([P, V // 2], F32, name="passed")
+        passed = keep.tile([P, V], F32, name="passed")
 
         def gate_arg(b, d, v0=0, v1=V):
             nc.vector.tensor_tensor(
                 arg[b][d][:, v0:v1], res[b][E][:].indirect(offsets(pos_sb[d], v0, v1)), centre[b][:, v0:v1], ADD
             )
 
-        def squash(b, d):
-            nc.scalar.activation(gate[b][d][:], arg[b][d][:], SIGMOID)
+        def squash(b, d, v0=0, v1=V):
+            nc.scalar.activation(gate[b][d][:, v0:v1], arg[b][d][:, v0:v1], SIGMOID)
 
         def gated(b, d, v0=0, v1=V):
             nc.vector.tensor_tensor(
                 term[b][d][:, v0:v1], res[b][H][:].indirect(offsets(pos_sb[d], v0, v1)), gate[b][d][:, v0:v1], MULT
             )
 
-        for v0, v1 in halves:
+        quarters = ((0, V // 4), (V // 4, V // 2))
+        for v0, v1 in quarters:
             nc.vector.tensor_copy(centre[0][:, v0:v1], res[0][Y][:].indirect(offsets(cen_sb, v0, v1)))
+        nc.scalar.activation(centre[0][:, V // 2 : V], res[0][Y][:].indirect(offsets(cen_sb, V // 2, V)), COPY)
         product_in_halves(0, H, 5)
-        for v0, v1 in halves:
+        for v0, v1 in quarters + halves[1:]:
             gate_arg(0, 0, v0, v1)
         product(1, Y, (0, HALF), 1)
-        product(1, Y, CUTS[2:], 2)
         squash(0, 0)
-        product(1, E, (0, HALF), 3)
+        product(1, Y, CUTS[2:], 2)
         gate_arg(0, 1)
         squash(0, 1)
+        product(1, E, (0, HALF), 3)
         nc.scalar.activation(centre[1][:], res[1][Y][:].indirect(cen_sb[:]), COPY)
-        product(1, E, CUTS[2:], 4)
+        product(1, E, CUTS[2:4], 4)
         gated(0, 0)
+        product(1, E, CUTS[3:6], 7, on_vector=True)
         for v0, v1 in halves:
             gated(0, 1, v0, v1)
         for v0, v1 in halves:
             nc.vector.tensor_tensor(z[0][:, v0:v1], term[0][0][:, v0:v1], term[0][1][:, v0:v1], ADD)
         nc.sync.dma_start(out[0:P, :], z[0][:])
-        product(1, H, (0, HALF), 7)
-        product(1, H, CUTS[2:], 0)
+        product(1, H, (0, HALF), 0)
+        product(1, H, CUTS[2:], 5)
 
         def fetch_passed(v0, v1):
             nc.scalar.activation(passed[:, v0:v1], res[1][H][:].indirect(offsets(pos_sb[1], v0, v1)), COPY)
 
-        gate_arg(1, 0)
-        squash(1, 0)
+        for v0, v1 in halves:
+            gate_arg(1, 0, v0, v1)
+        squash(1, 0, *halves[0])
         fetch_passed(*halves[0])
+        squash(1, 0, *halves[1])
+        fetch_passed(*halves[1])
         gate_arg(1, 1)
         squash(1, 1)
-        gated(1, 0)
-        gated(1, 1, *halves[1])
-        v0, v1 = halves[0]
-        nc.vector.tensor_tensor(term[1][1][:, v0:v1], passed[:, v0:v1], gate[1][1][:, v0:v1], MULT)
-        for queue, (v0, v1) in zip((nc.sync, nc.scalar), reversed(halves)):
+        for v0, v1 in halves:
+            gated(1, 0, v0, v1)
+        for v0, v1 in halves:
+            nc.vector.tensor_tensor(term[1][1][:, v0:v1], passed[:, v0:v1], gate[1][1][:, v0:v1], MULT)
+        for queue, (v0, v1) in zip((nc.sync, nc.scalar), halves):
             nc.vector.tensor_tensor(z[1][:, v0:v1], term[1][0][:, v0:v1], term[1][1][:, v0:v1], ADD)
             queue.dma_start(out[P : 2 * P, v0:v1], z[1][:, v0:v1])

@@ -34,6 +34,9 @@ LAST_CHUNKS = (
 )
 CUTS = (0, 256, 512, 768, 896, 1024)
 LAST_PIECE = CUTS[-2]
+THIN = 32
+WARM_PASSES = 4
+WARM_AT = 1280
 W_SCALE_AT = ((0, 0), (8, 0), (0, N))
 LAST_SCALE_AT = (4, P)
 
@@ -55,7 +58,7 @@ def tile_picked_gatedg_none_e_kernel(
 
         rows = xT.rearrange("(p j) t -> p j t", j=PACK)
         plane = [keep.tile([P, T], F32, name="plane%d" % j) for j in range(PACK)]
-        last_bf = keep.tile([P, T], BF16, name="last_bf")
+        last_bf = keep.tile([P, T], BF16, name="last_bf", align_bytes=64)
 
         warm_in = keep.tile([P, 1], F32, name="warm_in")
         warm_out = keep.tile([P, 1], F32, name="warm_out")
@@ -102,11 +105,42 @@ def tile_picked_gatedg_none_e_kernel(
         for j in range(PACK - 1):
             for u in range(2):
                 nc.vector.tensor_copy(picked[u][:, :, j], plane[j][:].indirect(offs_half[u]))
+        warm_bf = keep.tile([P, 2 * HALF], BF16, name="warm_bf", align_bytes=64)
+        warm_codes = keep.tile([P, BANK], U32, name="warm_codes", align_bytes=64)
+        warm_scale = keep.tile([P, BANK], U8, name="warm_scale", align_bytes=64)
+        thin_codes = keep.tile([P, THIN], U32, name="thin_codes", align_bytes=64)
+        thin_scale = keep.tile([P, THIN], U8, name="thin_scale", align_bytes=64)
+        nc.scalar.activation(warm_bf[:], plane[0][:, 0 : 2 * HALF], COPY)
+        for c0 in (0, BANK // 2):
+            nc.vector.quantize_mx(
+                out=warm_codes[:, c0 : c0 + BANK // 2].bitcast(FP8X4),
+                scales=warm_scale[:, c0 : c0 + BANK // 2],
+                in_=warm_bf[:],
+            )
+
+        def warm_up(c0):
+            nc.vector.quantize_mx(
+                out=thin_codes[:].bitcast(FP8X4), scales=thin_scale[:], in_=last_bf[:, c0 : c0 + PACK * THIN]
+            )
+            acc = bank_tile(7)
+            for n in range(WARM_PASSES):
+                nc.tensor.matmul_mx(
+                    out=acc[0:THIN, :],
+                    lhsT=thin_codes[:].bitcast(FP8X4),
+                    lhsT_scale=thin_scale[:],
+                    rhs=warm_codes[:].bitcast(FP8X4),
+                    rhs_scale=warm_scale[:],
+                    start=True,
+                    stop=True,
+                )
+
         for c0, c1, engine in LAST_CHUNKS:
             if engine == "scalar":
                 nc.scalar.activation(last_bf[:, c0:c1], plane[3][:, c0:c1], COPY)
             else:
                 nc.vector.tensor_copy(last_bf[:, c0:c1], plane[3][:, c0:c1])
+            if c0 == WARM_AT:
+                warm_up(c0)
         nc.vector.tensor_copy(picked[0][:, :, 3], plane[3][:].indirect(offs_half[0]))
         nc.scalar.activation(picked[1][:, :, 3], last_bf[:].indirect(offs_half[1]), COPY)
 

@@ -24,19 +24,11 @@ BANK = 512
 HALF = S // 2
 Y, E, H = 0, 1, 2
 
-LAST_CHUNKS = (
-    (0, 1280, "scalar"),
-    (1280, 2304, "scalar"),
-    (2304, 3328, "vector"),
-    (3328, 3712, "scalar"),
-    (3712, 3968, "vector"),
-    (3968, 4096, "scalar"),
-)
+LAST_PARTS = ((0, 3072), (3072, T))
 CUTS = (0, 256, 512, 768, 896, 1024)
 LAST_PIECE = CUTS[-2]
 THIN = 32
 WARM_PASSES = 4
-WARM_AT = 1280
 W_SCALE_AT = ((0, 0), (8, 0), (0, N))
 LAST_SCALE_AT = (4, P)
 
@@ -58,7 +50,6 @@ def tile_picked_gatedg_none_e_kernel(
 
         rows = xT.rearrange("(p j) t -> p j t", j=PACK)
         plane = [keep.tile([P, T], F32, name="plane%d" % j) for j in range(PACK)]
-        last_bf = keep.tile([P, T], BF16, name="last_bf", align_bytes=64)
 
         warm_in = keep.tile([P, 1], F32, name="warm_in")
         warm_out = keep.tile([P, 1], F32, name="warm_out")
@@ -92,7 +83,7 @@ def tile_picked_gatedg_none_e_kernel(
         load_scales(5, 11)
         nc.sync.dma_start(plane[2][:], rows[:, 2, :])
         load_scales(11, 12)
-        for c0, c1, engine in LAST_CHUNKS:
+        for c0, c1 in LAST_PARTS:
             nc.sync.dma_start(plane[3][:, c0:c1], rows[:, 3, c0:c1])
         for i in (Y, E, H):
             nc.sync.dma_start(w_words[i].bitcast(I32), words_in[i][0].rearrange("p n t -> p (n t)").bitcast(I32))
@@ -102,9 +93,20 @@ def tile_picked_gatedg_none_e_kernel(
 
         picked = [keep.tile([P, HALF, PACK], BF16, name="picked%d" % u, align_bytes=64) for u in range(2)]
         offs_half = [offs_sb[:, u * (HALF // LIST_ROWS) : (u + 1) * (HALF // LIST_ROWS)] for u in range(2)]
-        for j in range(PACK - 1):
+        flat = [keep.tile([P, HALF], BF16, name="flat%d" % j) for j in range(2)]
+
+        def scalar_half(j, pieces, weaves):
+            for n0, n1 in pieces:
+                offs_piece = offs_sb[:, (HALF + n0) // LIST_ROWS : (HALF + n1) // LIST_ROWS]
+                nc.scalar.activation(flat[j - 2][:, n0:n1], plane[j][:].indirect(offs_piece), COPY)
+            for n0, n1 in weaves:
+                nc.scalar.activation(picked[1][:, n0:n1, j], flat[j - 2][:, n0:n1], COPY)
+
+        for j in range(2):
             for u in range(2):
                 nc.vector.tensor_copy(picked[u][:, :, j], plane[j][:].indirect(offs_half[u]))
+        nc.vector.tensor_copy(picked[0][:, :, 2], plane[2][:].indirect(offs_half[0]))
+        scalar_half(2, ((0, HALF),), ((0, HALF),))
         warm_bf = keep.tile([P, 2 * HALF], BF16, name="warm_bf", align_bytes=64)
         warm_codes = keep.tile([P, BANK], U32, name="warm_codes", align_bytes=64)
         warm_scale = keep.tile([P, BANK], U8, name="warm_scale", align_bytes=64)
@@ -118,31 +120,24 @@ def tile_picked_gatedg_none_e_kernel(
                 in_=warm_bf[:],
             )
 
-        def warm_up(c0):
-            nc.vector.quantize_mx(
-                out=thin_codes[:].bitcast(FP8X4), scales=thin_scale[:], in_=last_bf[:, c0 : c0 + PACK * THIN]
+        thin_bf = keep.tile([P, PACK * THIN], BF16, name="thin_bf", align_bytes=64)
+        nc.scalar.activation(thin_bf[:], plane[3][:, 0 : PACK * THIN], COPY)
+        nc.vector.quantize_mx(out=thin_codes[:].bitcast(FP8X4), scales=thin_scale[:], in_=thin_bf[:])
+        warm_acc = bank_tile(7)
+        for n in range(WARM_PASSES):
+            nc.tensor.matmul_mx(
+                out=warm_acc[0:THIN, :],
+                lhsT=thin_codes[:].bitcast(FP8X4),
+                lhsT_scale=thin_scale[:],
+                rhs=warm_codes[:].bitcast(FP8X4),
+                rhs_scale=warm_scale[:],
+                start=True,
+                stop=True,
             )
-            acc = bank_tile(7)
-            for n in range(WARM_PASSES):
-                nc.tensor.matmul_mx(
-                    out=acc[0:THIN, :],
-                    lhsT=thin_codes[:].bitcast(FP8X4),
-                    lhsT_scale=thin_scale[:],
-                    rhs=warm_codes[:].bitcast(FP8X4),
-                    rhs_scale=warm_scale[:],
-                    start=True,
-                    stop=True,
-                )
 
-        for c0, c1, engine in LAST_CHUNKS:
-            if engine == "scalar":
-                nc.scalar.activation(last_bf[:, c0:c1], plane[3][:, c0:c1], COPY)
-            else:
-                nc.vector.tensor_copy(last_bf[:, c0:c1], plane[3][:, c0:c1])
-            if c0 == WARM_AT:
-                warm_up(c0)
         nc.vector.tensor_copy(picked[0][:, :, 3], plane[3][:].indirect(offs_half[0]))
-        nc.scalar.activation(picked[1][:, :, 3], last_bf[:].indirect(offs_half[1]), COPY)
+        late_cuts = [c - HALF for c in CUTS[2:]]
+        scalar_half(3, ((0, HALF // 2), (HALF // 2, HALF)), zip(late_cuts[:-1], late_cuts[1:]))
 
         codes = keep.tile([P, S], U32, name="codes", align_bytes=64)
         x_scale_tile = keep.tile([P, S], U8, name="x_scale_tile", align_bytes=64)

@@ -24,9 +24,10 @@ BANK = 512
 HALF = S // 2
 Y, E, H = 0, 1, 2
 
-LAST_PARTS = ((0, 3072), (3072, T))
+LAST_PARTS = ((0, 3584), (3584, T))
 CUTS = (0, 256, 512, 768, 896, 1024)
 LAST_PIECE = CUTS[-2]
+WOVEN = 128
 THIN = 32
 WARM_PASSES = 4
 W_SCALE_AT = ((0, 0), (8, 0), (0, N))
@@ -95,18 +96,19 @@ def tile_picked_gatedg_none_e_kernel(
         offs_half = [offs_sb[:, u * (HALF // LIST_ROWS) : (u + 1) * (HALF // LIST_ROWS)] for u in range(2)]
         flat = [keep.tile([P, HALF], BF16, name="flat%d" % j) for j in range(2)]
 
-        def scalar_half(j, pieces, weaves):
+        def second_half(j, pieces):
             for n0, n1 in pieces:
                 offs_piece = offs_sb[:, (HALF + n0) // LIST_ROWS : (HALF + n1) // LIST_ROWS]
                 nc.scalar.activation(flat[j - 2][:, n0:n1], plane[j][:].indirect(offs_piece), COPY)
-            for n0, n1 in weaves:
-                nc.scalar.activation(picked[1][:, n0:n1, j], flat[j - 2][:, n0:n1], COPY)
+            nc.vector.tensor_copy(picked[1][:, 0:WOVEN, j], flat[j - 2][:, 0:WOVEN])
+            for n0 in range(WOVEN, HALF, WOVEN):
+                nc.scalar.activation(picked[1][:, n0 : n0 + WOVEN, j], flat[j - 2][:, n0 : n0 + WOVEN], COPY)
 
         for j in range(2):
             for u in range(2):
                 nc.vector.tensor_copy(picked[u][:, :, j], plane[j][:].indirect(offs_half[u]))
         nc.vector.tensor_copy(picked[0][:, :, 2], plane[2][:].indirect(offs_half[0]))
-        scalar_half(2, ((0, HALF),), ((0, HALF),))
+        second_half(2, ((0, HALF),))
         warm_bf = keep.tile([P, 2 * HALF], BF16, name="warm_bf", align_bytes=64)
         warm_codes = keep.tile([P, BANK], U32, name="warm_codes", align_bytes=64)
         warm_scale = keep.tile([P, BANK], U8, name="warm_scale", align_bytes=64)
@@ -136,8 +138,7 @@ def tile_picked_gatedg_none_e_kernel(
             )
 
         nc.vector.tensor_copy(picked[0][:, :, 3], plane[3][:].indirect(offs_half[0]))
-        late_cuts = [c - HALF for c in CUTS[2:]]
-        scalar_half(3, ((0, HALF // 2), (HALF // 2, HALF)), zip(late_cuts[:-1], late_cuts[1:]))
+        second_half(3, ((0, WOVEN), (WOVEN, 2 * WOVEN), (2 * WOVEN, HALF)))
 
         codes = keep.tile([P, S], U32, name="codes", align_bytes=64)
         x_scale_tile = keep.tile([P, S], U8, name="x_scale_tile", align_bytes=64)

@@ -94,21 +94,19 @@ def tile_picked_gatedg_none_e_kernel(
 
         picked = [keep.tile([P, HALF, PACK], BF16, name="picked%d" % u, align_bytes=64) for u in range(2)]
         offs_half = [offs_sb[:, u * (HALF // LIST_ROWS) : (u + 1) * (HALF // LIST_ROWS)] for u in range(2)]
-        flat = [keep.tile([P, HALF], BF16, name="flat%d" % j) for j in range(2)]
+        flat = [keep.tile([P, HALF], BF16, name="flat%d" % j) for j in range(PACK)]
 
-        def second_half(j, pieces):
-            for n0, n1 in pieces:
-                offs_piece = offs_sb[:, (HALF + n0) // LIST_ROWS : (HALF + n1) // LIST_ROWS]
-                nc.scalar.activation(flat[j - 2][:, n0:n1], plane[j][:].indirect(offs_piece), COPY)
-            nc.vector.tensor_copy(picked[1][:, 0:WOVEN, j], flat[j - 2][:, 0:WOVEN])
-            for n0 in range(WOVEN, HALF, WOVEN):
-                nc.scalar.activation(picked[1][:, n0 : n0 + WOVEN, j], flat[j - 2][:, n0 : n0 + WOVEN], COPY)
+        def fetch_flat(j, n0, n1):
+            offs_piece = offs_sb[:, (HALF + n0) // LIST_ROWS : (HALF + n1) // LIST_ROWS]
+            nc.scalar.activation(flat[j][:, n0:n1], plane[j][:].indirect(offs_piece), COPY)
 
-        for j in range(2):
-            for u in range(2):
-                nc.vector.tensor_copy(picked[u][:, :, j], plane[j][:].indirect(offs_half[u]))
-        nc.vector.tensor_copy(picked[0][:, :, 2], plane[2][:].indirect(offs_half[0]))
-        second_half(2, ((0, HALF),))
+        def weave(j, n0, n1):
+            nc.scalar.activation(picked[1][:, n0:n1, j], flat[j][:, n0:n1], COPY)
+
+        for j in range(PACK - 1):
+            nc.vector.tensor_copy(picked[0][:, :, j], plane[j][:].indirect(offs_half[0]))
+            fetch_flat(j, 0, HALF)
+            weave(j, 0, HALF)
         warm_bf = keep.tile([P, 2 * HALF], BF16, name="warm_bf", align_bytes=64)
         warm_codes = keep.tile([P, BANK], U32, name="warm_codes", align_bytes=64)
         warm_scale = keep.tile([P, BANK], U8, name="warm_scale", align_bytes=64)
@@ -138,7 +136,11 @@ def tile_picked_gatedg_none_e_kernel(
             )
 
         nc.vector.tensor_copy(picked[0][:, :, 3], plane[3][:].indirect(offs_half[0]))
-        second_half(3, ((0, WOVEN), (WOVEN, 2 * WOVEN), (2 * WOVEN, HALF)))
+        for n0, n1 in ((0, WOVEN), (WOVEN, 2 * WOVEN), (2 * WOVEN, HALF)):
+            fetch_flat(3, n0, n1)
+        nc.gpsimd.tensor_copy(picked[1][:, 0:WOVEN, 3], flat[3][:, 0:WOVEN])
+        for n0 in range(WOVEN, HALF, WOVEN):
+            weave(3, n0, n0 + WOVEN)
 
         codes = keep.tile([P, S], U32, name="codes", align_bytes=64)
         x_scale_tile = keep.tile([P, S], U8, name="x_scale_tile", align_bytes=64)

@@ -25,9 +25,8 @@ HALF = S // 2
 Y, E, H = 0, 1, 2
 
 LAST_PARTS = ((0, 3584), (3584, T))
-CUTS = (0, 256, 512, 768, 896, 1024)
-LAST_PIECE = CUTS[-2]
 WOVEN = 128
+LOW, HIGH, MID, LATE, LAST = (0, 256), (256, 512), (512, 768), (768, 896), (896, 1024)
 THIN = 32
 WARM_PASSES = 4
 W_SCALE_AT = ((0, 0), (8, 0), (0, N))
@@ -45,6 +44,9 @@ def tile_picked_gatedg_none_e_kernel(
         def bank_tile(bank):
             return psum.tile([P, BANK], F32, name="acc", tag="bank%d" % bank)
 
+        def offsets(list_sb, n0, n1):
+            return list_sb[:, n0 // LIST_ROWS : n1 // LIST_ROWS]
+
         offs_sb = keep.tile([P, S // LIST_ROWS], U16, name="offs_sb")
         cen_sb = keep.tile([P, V // LIST_ROWS], U16, name="cen_sb")
         pos_sb = [keep.tile([P, V // LIST_ROWS], U16, name="pos%d_sb" % d) for d in range(2)]
@@ -57,16 +59,15 @@ def tile_picked_gatedg_none_e_kernel(
         nc.vector.memset(warm_in[:], 0.0)
         nc.scalar.activation(warm_out[:], warm_in[:], SIGMOID)
 
-        w_tiles = [keep.tile([P, N], U32, name="w_words%d" % i, align_bytes=64) for i in (Y, E, H)]
-        w_words = [tile[:] for tile in w_tiles]
+        w_words = [keep.tile([P, N], U32, name="w_words%d" % i, align_bytes=64) for i in (Y, E, H)]
         scale_tile = keep.tile([P, 2 * N], U8, name="scale_tile", align_bytes=64)
         nc.vector.memset(scale_tile[:].bitcast(I32), 0)
         words_in = (w1_words, w2_words, w3_words)
         scales_in = (w1_scales, w2_scales, w3_scales)
 
-        def w_scale(i, c0, c1):
+        def w_scale(i, b):
             row, col = W_SCALE_AT[i]
-            return scale_tile[row:P, col + c0 : col + c1]
+            return scale_tile[row:P, col + b * P : col + (b + 1) * P]
 
         def load_scales(first, last):
             for n in range(first, last):
@@ -87,29 +88,32 @@ def tile_picked_gatedg_none_e_kernel(
         for c0, c1 in LAST_PARTS:
             nc.sync.dma_start(plane[3][:, c0:c1], rows[:, 3, c0:c1])
         for i in (Y, E, H):
-            nc.sync.dma_start(w_words[i].bitcast(I32), words_in[i][0].rearrange("p n t -> p (n t)").bitcast(I32))
+            nc.sync.dma_start(w_words[i][:].bitcast(I32), words_in[i][0].rearrange("p n t -> p (n t)").bitcast(I32))
         nc.sync.dma_start(cen_sb[:], cen)
         nc.sync.dma_start(pos_sb[0][:], pos1)
         nc.sync.dma_start(pos_sb[1][:], pos2)
 
         picked = [keep.tile([P, HALF, PACK], BF16, name="picked%d" % u, align_bytes=64) for u in range(2)]
-        offs_half = [offs_sb[:, u * (HALF // LIST_ROWS) : (u + 1) * (HALF // LIST_ROWS)] for u in range(2)]
         flat = [keep.tile([P, HALF], BF16, name="flat%d" % j) for j in range(PACK)]
 
+        def fetch_stepped(j):
+            nc.vector.tensor_copy(picked[0][:, :, j], plane[j][:].indirect(offsets(offs_sb, 0, HALF)))
+
         def fetch_flat(j, n0, n1):
-            offs_piece = offs_sb[:, (HALF + n0) // LIST_ROWS : (HALF + n1) // LIST_ROWS]
-            nc.scalar.activation(flat[j][:, n0:n1], plane[j][:].indirect(offs_piece), COPY)
+            nc.scalar.activation(flat[j][:, n0:n1], plane[j][:].indirect(offsets(offs_sb, HALF + n0, HALF + n1)), COPY)
 
         def weave(j, n0, n1):
             nc.scalar.activation(picked[1][:, n0:n1, j], flat[j][:, n0:n1], COPY)
 
         for j in range(PACK - 1):
-            nc.vector.tensor_copy(picked[0][:, :, j], plane[j][:].indirect(offs_half[0]))
+            fetch_stepped(j)
             fetch_flat(j, 0, HALF)
             weave(j, 0, HALF)
+
         warm_bf = keep.tile([P, 2 * HALF], BF16, name="warm_bf", align_bytes=64)
         warm_codes = keep.tile([P, BANK], U32, name="warm_codes", align_bytes=64)
         warm_scale = keep.tile([P, BANK], U8, name="warm_scale", align_bytes=64)
+        thin_bf = keep.tile([P, PACK * THIN], BF16, name="thin_bf", align_bytes=64)
         thin_codes = keep.tile([P, THIN], U32, name="thin_codes", align_bytes=64)
         thin_scale = keep.tile([P, THIN], U8, name="thin_scale", align_bytes=64)
         nc.scalar.activation(warm_bf[:], plane[0][:, 0 : 2 * HALF], COPY)
@@ -119,8 +123,6 @@ def tile_picked_gatedg_none_e_kernel(
                 scales=warm_scale[:, c0 : c0 + BANK // 2],
                 in_=warm_bf[:],
             )
-
-        thin_bf = keep.tile([P, PACK * THIN], BF16, name="thin_bf", align_bytes=64)
         nc.scalar.activation(thin_bf[:], plane[3][:, 0 : PACK * THIN], COPY)
         nc.vector.quantize_mx(out=thin_codes[:].bitcast(FP8X4), scales=thin_scale[:], in_=thin_bf[:])
         warm_acc = bank_tile(7)
@@ -135,25 +137,24 @@ def tile_picked_gatedg_none_e_kernel(
                 stop=True,
             )
 
-        nc.vector.tensor_copy(picked[0][:, :, 3], plane[3][:].indirect(offs_half[0]))
+        fetch_stepped(3)
         for n0, n1 in ((0, WOVEN), (WOVEN, 2 * WOVEN), (2 * WOVEN, HALF)):
             fetch_flat(3, n0, n1)
-        nc.gpsimd.tensor_copy(picked[1][:, 0:WOVEN, 3], flat[3][:, 0:WOVEN])
+        nc.gpsimd.tensor_scalar(picked[1][:, 0:WOVEN, 3], flat[3][:, 0:WOVEN], 1.0, 0.0, op0=MULT, op1=ADD)
         for n0 in range(WOVEN, HALF, WOVEN):
             weave(3, n0, n0 + WOVEN)
 
         codes = keep.tile([P, S], U32, name="codes", align_bytes=64)
         x_scale_tile = keep.tile([P, S], U8, name="x_scale_tile", align_bytes=64)
-
         res = [[keep.tile([P, S], F32, name="res%d_%d" % (b, i)) for i in (Y, E, H)] for b in range(2)]
 
         def x_scale(c0, c1):
-            if c0 >= LAST_PIECE:
+            if c0 >= LAST[0]:
                 row, col = LAST_SCALE_AT
-                return scale_tile[row:P, col + c0 - LAST_PIECE : col + c1 - LAST_PIECE]
+                return scale_tile[row:P, col + c0 - LAST[0] : col + c1 - LAST[0]]
             return x_scale_tile[:, c0:c1]
 
-        for c0, c1 in zip(CUTS[:-1], CUTS[1:]):
+        for c0, c1 in (LOW, HIGH, MID, LATE, LAST):
             u = c0 // HALF
             nc.vector.quantize_mx(
                 out=codes[:, c0:c1].bitcast(FP8X4),
@@ -161,49 +162,46 @@ def tile_picked_gatedg_none_e_kernel(
                 in_=picked[u][:, c0 - u * HALF : c1 - u * HALF, :].rearrange("p n j -> p (n j)"),
             )
 
-        def product(b, i, cuts, bank, on_vector=False):
-            c0, c1 = cuts[0], cuts[-1]
-            acc = bank_tile(bank)
+        def passes(acc, at, b, i, cuts):
             for a0, a1 in zip(cuts[:-1], cuts[1:]):
                 nc.tensor.matmul_mx(
-                    out=acc[:, a0 - c0 : a1 - c0],
+                    out=acc[:, at + a0 - cuts[0] : at + a1 - cuts[0]],
                     lhsT=w_words[i][:, b * P : (b + 1) * P].bitcast(FP8X4),
-                    lhsT_scale=w_scale(i, b * P, (b + 1) * P),
+                    lhsT_scale=w_scale(i, b),
                     rhs=codes[:, a0:a1].bitcast(FP8X4),
                     rhs_scale=x_scale(a0, a1),
                     start=True,
                     stop=True,
                 )
-            dst = res[b][i][:, c0:c1]
+
+        def empty(acc, at, b, i, c0, c1, on_vector=False):
             if on_vector:
-                nc.vector.tensor_copy(dst, acc[:, 0 : c1 - c0])
+                nc.vector.tensor_copy(res[b][i][:, c0:c1], acc[:, at : at + c1 - c0])
             else:
-                nc.scalar.activation(dst, acc[:, 0 : c1 - c0], COPY)
+                nc.scalar.activation(res[b][i][:, c0:c1], acc[:, at : at + c1 - c0], COPY)
 
-        def product_in_halves(b, i, bank):
-            product(b, i, (0, HALF), bank)
-            product(b, i, CUTS[2:], bank + 1)
+        def product(b, i, cuts, bank, on_vector=False):
+            acc = bank_tile(bank)
+            passes(acc, 0, b, i, cuts)
+            empty(acc, 0, b, i, cuts[0], cuts[-1], on_vector)
 
-        product(0, Y, CUTS[0:2], 0)
-        product(0, E, CUTS[0:2], 1)
-        product(0, Y, CUTS[1:3], 2)
-        product(0, E, CUTS[1:3], 3)
-        product(0, Y, CUTS[2:4], 4, on_vector=True)
-        product(0, Y, CUTS[3:5], 5, on_vector=True)
-        product(0, Y, CUTS[4:6], 6)
-        product(0, E, CUTS[2:4], 7, on_vector=True)
-        product(0, E, CUTS[3:6], 0)
+        LOWER = (0, HALF)
+        UPPER = (HALF, 768, 896, S)
         halves = ((0, V // 2), (V // 2, V))
-
-        def offsets(list_sb, v0, v1):
-            return list_sb[:, v0 // LIST_ROWS : v1 // LIST_ROWS]
-
+        quarters = ((0, V // 4), (V // 4, V // 2))
         centre = [keep.tile([P, V], F32, name="centre%d" % b) for b in range(2)]
         arg = [[keep.tile([P, V], F32, name="arg%d_%d" % (b, d)) for d in range(2)] for b in range(2)]
         gate = [[keep.tile([P, V], F32, name="gate%d_%d" % (b, d)) for d in range(2)] for b in range(2)]
         term = [[keep.tile([P, V], F32, name="term%d_%d" % (b, d)) for d in range(2)] for b in range(2)]
         z = [keep.tile([P, V], F32, name="z%d" % b) for b in range(2)]
-        passed = keep.tile([P, V], F32, name="passed")
+        passed = [None, keep.tile([P, V], F32, name="passed1")]
+
+        def fetch_centre(b, v0, v1, on_vector):
+            window = res[b][Y][:].indirect(offsets(cen_sb, v0, v1))
+            if on_vector:
+                nc.vector.tensor_copy(centre[b][:, v0:v1], window)
+            else:
+                nc.scalar.activation(centre[b][:, v0:v1], window, COPY)
 
         def gate_arg(b, d, v0=0, v1=V):
             nc.vector.tensor_tensor(
@@ -218,46 +216,59 @@ def tile_picked_gatedg_none_e_kernel(
                 term[b][d][:, v0:v1], res[b][H][:].indirect(offsets(pos_sb[d], v0, v1)), gate[b][d][:, v0:v1], MULT
             )
 
-        quarters = ((0, V // 4), (V // 4, V // 2))
+        def fetch_passed(d, v0, v1):
+            nc.scalar.activation(passed[d][:, v0:v1], res[1][H][:].indirect(offsets(pos_sb[d], v0, v1)), COPY)
+
+        def times_gate(d, v0, v1):
+            nc.vector.tensor_tensor(term[1][d][:, v0:v1], passed[d][:, v0:v1], gate[1][d][:, v0:v1], MULT)
+
+        def add_terms(engine, b, v0, v1):
+            engine.tensor_tensor(z[b][:, v0:v1], term[b][0][:, v0:v1], term[b][1][:, v0:v1], ADD)
+
+        product(0, Y, LOW, 0)
+        product(0, E, LOW, 1)
+        product(0, Y, HIGH, 2)
+        product(0, E, HIGH, 3)
+        product(0, Y, MID, 4, on_vector=True)
+        product(0, Y, LATE, 5, on_vector=True)
+        product(0, Y, LAST, 6)
+        product(0, E, MID, 7, on_vector=True)
+        product(0, E, UPPER[1:], 0)
         for v0, v1 in quarters:
-            nc.vector.tensor_copy(centre[0][:, v0:v1], res[0][Y][:].indirect(offsets(cen_sb, v0, v1)))
-        nc.scalar.activation(centre[0][:, V // 2 : V], res[0][Y][:].indirect(offsets(cen_sb, V // 2, V)), COPY)
-        product_in_halves(0, H, 5)
+            fetch_centre(0, v0, v1, True)
+        fetch_centre(0, V // 2, V, False)
+        product(0, H, LOWER, 5)
+        product(0, H, UPPER, 6)
         for v0, v1 in quarters + halves[1:]:
             gate_arg(0, 0, v0, v1)
-        product(1, Y, (0, HALF), 1)
+        product(1, Y, LOWER, 1)
         squash(0, 0)
-        product(1, Y, CUTS[2:], 2)
+        product(1, Y, UPPER, 2)
         gate_arg(0, 1)
         squash(0, 1)
-        product(1, E, (0, HALF), 3)
-        nc.scalar.activation(centre[1][:], res[1][Y][:].indirect(cen_sb[:]), COPY)
-        product(1, E, CUTS[2:4], 4)
+        product(1, E, LOWER, 3)
+        fetch_centre(1, 0, V, False)
+        product(1, E, UPPER[0:2], 4)
         gated(0, 0)
-        product(1, E, CUTS[3:6], 7, on_vector=True)
+        product(1, E, UPPER[1:], 7, on_vector=True)
         for v0, v1 in halves:
             gated(0, 1, v0, v1)
         for v0, v1 in halves:
-            nc.vector.tensor_tensor(z[0][:, v0:v1], term[0][0][:, v0:v1], term[0][1][:, v0:v1], ADD)
+            add_terms(nc.vector, 0, v0, v1)
         nc.sync.dma_start(out[0:P, :], z[0][:])
-        product(1, H, (0, HALF), 0)
-        product(1, H, CUTS[2:], 5)
-
-        def fetch_passed(v0, v1):
-            nc.scalar.activation(passed[:, v0:v1], res[1][H][:].indirect(offsets(pos_sb[1], v0, v1)), COPY)
-
+        product(1, H, LOWER, 0)
+        product(1, H, UPPER, 5)
         for v0, v1 in halves:
             gate_arg(1, 0, v0, v1)
-        squash(1, 0, *halves[0])
-        fetch_passed(*halves[0])
-        squash(1, 0, *halves[1])
-        fetch_passed(*halves[1])
+        for v0, v1 in halves:
+            squash(1, 0, v0, v1)
+            fetch_passed(1, v0, v1)
         gate_arg(1, 1)
         squash(1, 1)
         for v0, v1 in halves:
             gated(1, 0, v0, v1)
         for v0, v1 in halves:
-            nc.vector.tensor_tensor(term[1][1][:, v0:v1], passed[:, v0:v1], gate[1][1][:, v0:v1], MULT)
+            times_gate(1, v0, v1)
         for queue, (v0, v1) in zip((nc.sync, nc.scalar), halves):
-            nc.vector.tensor_tensor(z[1][:, v0:v1], term[1][0][:, v0:v1], term[1][1][:, v0:v1], ADD)
+            add_terms(nc.vector, 1, v0, v1)
             queue.dma_start(out[P : 2 * P, v0:v1], z[1][:, v0:v1])

@@ -25,7 +25,7 @@ HALF = S // 2
 Y, E, H = 0, 1, 2
 
 LAST_PARTS = ((0, 3584), (3584, T))
-WOVEN = 128
+WOVEN = 192
 LOW, HIGH, MID, LATE, LAST = (0, 256), (256, 512), (512, 768), (768, 896), (896, 1024)
 THIN = 32
 WARM_PASSES = 4
@@ -141,8 +141,8 @@ def tile_picked_gatedg_none_e_kernel(
         for n0, n1 in ((0, WOVEN), (WOVEN, 2 * WOVEN), (2 * WOVEN, HALF)):
             fetch_flat(3, n0, n1)
         nc.gpsimd.tensor_scalar(picked[1][:, 0:WOVEN, 3], flat[3][:, 0:WOVEN], 1.0, 0.0, op0=MULT, op1=ADD)
-        for n0 in range(WOVEN, HALF, WOVEN):
-            weave(3, n0, n0 + WOVEN)
+        weave(3, WOVEN, 2 * WOVEN)
+        weave(3, 2 * WOVEN, HALF)
 
         codes = keep.tile([P, S], U32, name="codes", align_bytes=64)
         x_scale_tile = keep.tile([P, S], U8, name="x_scale_tile", align_bytes=64)
@@ -248,9 +248,9 @@ def tile_picked_gatedg_none_e_kernel(
         squash(0, 1)
         product(1, E, LOWER, 3)
         fetch_centre(1, 0, V, False)
-        product(1, E, UPPER[0:2], 4)
+        product(1, E, UPPER[0:3], 4)
         gated(0, 0)
-        product(1, E, UPPER[1:], 7, on_vector=True)
+        product(1, E, UPPER[2:], 7, on_vector=True)
         for v0, v1 in halves:
             gated(0, 1, v0, v1)
         for v0, v1 in halves:

@@ -248,9 +248,9 @@ def tile_picked_gatedg_none_e_kernel(
         squash(0, 1)
         product(1, E, LOWER, 3)
         fetch_centre(1, 0, V, False)
-        product(1, E, UPPER[0:3], 4)
+        product(1, E, UPPER[0:2], 4)
         gated(0, 0)
-        product(1, E, UPPER[2:], 7, on_vector=True)
+        product(1, E, UPPER[1:], 7, on_vector=True)
         for v0, v1 in halves:
             gated(0, 1, v0, v1)
         for v0, v1 in halves:

@@ -228,10 +228,13 @@ def tile_picked_gatedg_none_e_kernel(
         product(0, Y, LOW, 0)
         product(0, E, LOW, 1)
         product(0, Y, HIGH, 2)
-        product(0, E, HIGH, 3)
+        shared = bank_tile(6)
+        passes(shared, P, 0, E, HIGH)
         product(0, Y, MID, 4, on_vector=True)
         product(0, Y, LATE, 5, on_vector=True)
-        product(0, Y, LAST, 6)
+        passes(shared, 0, 0, Y, LAST)
+        empty(shared, 0, 0, Y, *LAST)
+        empty(shared, P, 0, E, *HIGH)
         product(0, E, MID, 7, on_vector=True)
         product(0, E, UPPER[1:], 0)
         for v0, v1 in quarters:

from contextlib import ExitStack

import concourse.mybir as mybir

K, T, S, V, N = 512, 4096, 1024, 512, 256
FLOPS = 3 * 2 * K * N * S

F32 = mybir.dt.float32
BF16 = mybir.dt.bfloat16
I32 = mybir.dt.int32
U32 = mybir.dt.uint32
U16 = mybir.dt.uint16
U8 = mybir.dt.uint8
FP8X4 = mybir.dt.float8_e4m3fn_x4
ADD = mybir.AluOpType.add
MULT = mybir.AluOpType.mult
COPY = mybir.ActivationFunctionType.Copy
SIGMOID = mybir.ActivationFunctionType.Sigmoid

P = 128
PACK = 4
LIST_ROWS = 16
BANK = 512
HALF = S // 2
Y, E, H = 0, 1, 2

LAST_PARTS = ((0, 3584), (3584, T))
WOVEN = 192
LOW, HIGH, MID, LATE, LAST = (0, 256), (256, 512), (512, 768), (768, 896), (896, 1024)
THIN = 32
WARM_PASSES = 4
W_SCALE_AT = ((0, 0), (8, 0), (0, N))
LAST_SCALE_AT = (4, P)


def tile_picked_gatedg_none_e_kernel(
    tc, xT, w1_words, w1_scales, w2_words, w2_scales, w3_words, w3_scales, offs, cen, pos1, pos2, out
):
    nc = tc.nc
    with ExitStack() as ctx:
        keep = ctx.enter_context(tc.tile_pool(name="keep", bufs=1))
        psum = ctx.enter_context(tc.psum_pool(name="psum", bufs=1))

        def bank_tile(bank):
            return psum.tile([P, BANK], F32, name="acc", tag="bank%d" % bank)

        def offsets(list_sb, n0, n1):
            return list_sb[:, n0 // LIST_ROWS : n1 // LIST_ROWS]

        offs_sb = keep.tile([P, S // LIST_ROWS], U16, name="offs_sb")
        cen_sb = keep.tile([P, V // LIST_ROWS], U16, name="cen_sb")
        pos_sb = [keep.tile([P, V // LIST_ROWS], U16, name="pos%d_sb" % d) for d in range(2)]

        rows = xT.rearrange("(p j) t -> p j t", j=PACK)
        plane = [keep.tile([P, T], F32, name="plane%d" % j) for j in range(PACK)]

        warm_in = keep.tile([P, 1], F32, name="warm_in")
        warm_out = keep.tile([P, 1], F32, name="warm_out")
        nc.vector.memset(warm_in[:], 0.0)
        nc.scalar.activation(warm_out[:], warm_in[:], SIGMOID)

        w_words = [keep.tile([P, N], U32, name="w_words%d" % i, align_bytes=64) for i in (Y, E, H)]
        scale_tile = keep.tile([P, 2 * N], U8, name="scale_tile", align_bytes=64)
        nc.vector.memset(scale_tile[:].bitcast(I32), 0)
        words_in = (w1_words, w2_words, w3_words)
        scales_in = (w1_scales, w2_scales, w3_scales)

        def w_scale(i, b):
            row, col = W_SCALE_AT[i]
            return scale_tile[row:P, col + b * P : col + (b + 1) * P]

        def load_scales(first, last):
            for n in range(first, last):
                i, q = divmod(n, 4)
                row, col = W_SCALE_AT[i]
                nc.sync.dma_start(
                    scale_tile[32 * q + row : 32 * q + row + 4, col : col + N].bitcast(I32),
                    scales_in[i][0, 4 * q : 4 * q + 4, :].bitcast(I32),
                )

        nc.sync.dma_start(plane[0][:], rows[:, 0, :])
        nc.sync.dma_start(offs_sb[:], offs)
        load_scales(0, 5)
        nc.sync.dma_start(plane[1][:], rows[:, 1, :])
        load_scales(5, 11)
        nc.sync.dma_start(plane[2][:], rows[:, 2, :])
        load_scales(11, 12)
        for c0, c1 in LAST_PARTS:
            nc.sync.dma_start(plane[3][:, c0:c1], rows[:, 3, c0:c1])
        for i in (Y, E, H):
            nc.sync.dma_start(w_words[i][:].bitcast(I32), words_in[i][0].rearrange("p n t -> p (n t)").bitcast(I32))
        nc.sync.dma_start(cen_sb[:], cen)
        nc.sync.dma_start(pos_sb[0][:], pos1)
        nc.sync.dma_start(pos_sb[1][:], pos2)

        picked = [keep.tile([P, HALF, PACK], BF16, name="picked%d" % u, align_bytes=64) for u in range(2)]
        flat = [keep.tile([P, HALF], BF16, name="flat%d" % j) for j in range(PACK)]

        def fetch_stepped(j):
            nc.vector.tensor_copy(picked[0][:, :, j], plane[j][:].indirect(offsets(offs_sb, 0, HALF)))

        def fetch_flat(j, n0, n1):
            nc.scalar.activation(flat[j][:, n0:n1], plane[j][:].indirect(offsets(offs_sb, HALF + n0, HALF + n1)), COPY)

        def weave(j, n0, n1):
            nc.scalar.activation(picked[1][:, n0:n1, j], flat[j][:, n0:n1], COPY)

        for j in range(PACK - 1):
            fetch_stepped(j)
            fetch_flat(j, 0, HALF)
            weave(j, 0, HALF)

        warm_bf = keep.tile([P, 2 * HALF], BF16, name="warm_bf", align_bytes=64)
        warm_codes = keep.tile([P, BANK], U32, name="warm_codes", align_bytes=64)
        warm_scale = keep.tile([P, BANK], U8, name="warm_scale", align_bytes=64)
        thin_bf = keep.tile([P, PACK * THIN], BF16, name="thin_bf", align_bytes=64)
        thin_codes = keep.tile([P, THIN], U32, name="thin_codes", align_bytes=64)
        thin_scale = keep.tile([P, THIN], U8, name="thin_scale", align_bytes=64)
        nc.scalar.activation(warm_bf[:], plane[0][:, 0 : 2 * HALF], COPY)
        for c0 in (0, BANK // 2):
            nc.vector.quantize_mx(
                out=warm_codes[:, c0 : c0 + BANK // 2].bitcast(FP8X4),
                scales=warm_scale[:, c0 : c0 + BANK // 2],
                in_=warm_bf[:],
            )
        nc.scalar.activation(thin_bf[:], plane[3][:, 0 : PACK * THIN], COPY)
        nc.vector.quantize_mx(out=thin_codes[:].bitcast(FP8X4), scales=thin_scale[:], in_=thin_bf[:])
        warm_acc = bank_tile(7)
        for n in range(WARM_PASSES):
            nc.tensor.matmul_mx(
                out=warm_acc[0:THIN, :],
                lhsT=thin_codes[:].bitcast(FP8X4),
                lhsT_scale=thin_scale[:],
                rhs=warm_codes[:].bitcast(FP8X4),
                rhs_scale=warm_scale[:],
                start=True,
                stop=True,
            )

        fetch_stepped(3)
        for n0, n1 in ((0, WOVEN), (WOVEN, 2 * WOVEN), (2 * WOVEN, HALF)):
            fetch_flat(3, n0, n1)
        nc.gpsimd.tensor_scalar(picked[1][:, 0:WOVEN, 3], flat[3][:, 0:WOVEN], 1.0, 0.0, op0=MULT, op1=ADD)
        weave(3, WOVEN, 2 * WOVEN)
        weave(3, 2 * WOVEN, HALF)

        codes = keep.tile([P, S], U32, name="codes", align_bytes=64)
        x_scale_tile = keep.tile([P, S], U8, name="x_scale_tile", align_bytes=64)
        res = [[keep.tile([P, S], F32, name="res%d_%d" % (b, i)) for i in (Y, E, H)] for b in range(2)]

        def x_scale(c0, c1):
            if c0 >= LAST[0]:
                row, col = LAST_SCALE_AT
                return scale_tile[row:P, col + c0 - LAST[0] : col + c1 - LAST[0]]
            return x_scale_tile[:, c0:c1]

        for c0, c1 in (LOW, HIGH, MID, LATE, LAST):
            u = c0 // HALF
            nc.vector.quantize_mx(
                out=codes[:, c0:c1].bitcast(FP8X4),
                scales=x_scale(c0, c1),
                in_=picked[u][:, c0 - u * HALF : c1 - u * HALF, :].rearrange("p n j -> p (n j)"),
            )

        def passes(acc, at, b, i, cuts):
            for a0, a1 in zip(cuts[:-1], cuts[1:]):
                nc.tensor.matmul_mx(
                    out=acc[:, at + a0 - cuts[0] : at + a1 - cuts[0]],
                    lhsT=w_words[i][:, b * P : (b + 1) * P].bitcast(FP8X4),
                    lhsT_scale=w_scale(i, b),
                    rhs=codes[:, a0:a1].bitcast(FP8X4),
                    rhs_scale=x_scale(a0, a1),
                    start=True,
                    stop=True,
                )

        def empty(acc, at, b, i, c0, c1, on_vector=False):
            if on_vector:
                nc.vector.tensor_copy(res[b][i][:, c0:c1], acc[:, at : at + c1 - c0])
            else:
                nc.scalar.activation(res[b][i][:, c0:c1], acc[:, at : at + c1 - c0], COPY)

        def product(b, i, cuts, bank, on_vector=False):
            acc = bank_tile(bank)
            passes(acc, 0, b, i, cuts)
            empty(acc, 0, b, i, cuts[0], cuts[-1], on_vector)

        LOWER = (0, HALF)
        UPPER = (HALF, 768, 896, S)
        halves = ((0, V // 2), (V // 2, V))
        quarters = ((0, V // 4), (V // 4, V // 2))
        centre = [keep.tile([P, V], F32, name="centre%d" % b) for b in range(2)]
        arg = [[keep.tile([P, V], F32, name="arg%d_%d" % (b, d)) for d in range(2)] for b in range(2)]
        gate = [[keep.tile([P, V], F32, name="gate%d_%d" % (b, d)) for d in range(2)] for b in range(2)]
        term = [[keep.tile([P, V], F32, name="term%d_%d" % (b, d)) for d in range(2)] for b in range(2)]
        z = [keep.tile([P, V], F32, name="z%d" % b) for b in range(2)]
        passed = [None, keep.tile([P, V], F32, name="passed1")]

        def fetch_centre(b, v0, v1, on_vector):
            window = res[b][Y][:].indirect(offsets(cen_sb, v0, v1))
            if on_vector:
                nc.vector.tensor_copy(centre[b][:, v0:v1], window)
            else:
                nc.scalar.activation(centre[b][:, v0:v1], window, COPY)

        def gate_arg(b, d, v0=0, v1=V):
            nc.vector.tensor_tensor(
                arg[b][d][:, v0:v1], res[b][E][:].indirect(offsets(pos_sb[d], v0, v1)), centre[b][:, v0:v1], ADD
            )

        def squash(b, d, v0=0, v1=V):
            nc.scalar.activation(gate[b][d][:, v0:v1], arg[b][d][:, v0:v1], SIGMOID)

        def gated(b, d, v0=0, v1=V):
            nc.vector.tensor_tensor(
                term[b][d][:, v0:v1], res[b][H][:].indirect(offsets(pos_sb[d], v0, v1)), gate[b][d][:, v0:v1], MULT
            )

        def fetch_passed(d, v0, v1):
            nc.scalar.activation(passed[d][:, v0:v1], res[1][H][:].indirect(offsets(pos_sb[d], v0, v1)), COPY)

        def times_gate(d, v0, v1):
            nc.vector.tensor_tensor(term[1][d][:, v0:v1], passed[d][:, v0:v1], gate[1][d][:, v0:v1], MULT)

        def add_terms(engine, b, v0, v1):
            engine.tensor_tensor(z[b][:, v0:v1], term[b][0][:, v0:v1], term[b][1][:, v0:v1], ADD)

        product(0, Y, LOW, 0)
        product(0, E, LOW, 1)
        product(0, Y, HIGH, 2)
        shared = bank_tile(6)
        passes(shared, P, 0, E, HIGH)
        product(0, Y, MID, 4, on_vector=True)
        product(0, Y, LATE, 5, on_vector=True)
        passes(shared, 0, 0, Y, LAST)
        empty(shared, 0, 0, Y, *LAST)
        empty(shared, P, 0, E, *HIGH)
        product(0, E, MID, 7, on_vector=True)
        product(0, E, UPPER[1:], 0)
        for v0, v1 in quarters:
            fetch_centre(0, v0, v1, True)
        fetch_centre(0, V // 2, V, False)
        product(0, H, LOWER, 5)
        product(0, H, UPPER, 6)
        for v0, v1 in quarters + halves[1:]:
            gate_arg(0, 0, v0, v1)
        product(1, Y, LOWER, 1)
        squash(0, 0)
        product(1, Y, UPPER, 2)
        gate_arg(0, 1)
        squash(0, 1)
        product(1, E, LOWER, 3)
        fetch_centre(1, 0, V, False)
        product(1, E, UPPER[0:2], 4)
        gated(0, 0)
        product(1, E, UPPER[1:], 7, on_vector=True)
        for v0, v1 in halves:
            gated(0, 1, v0, v1)
        for v0, v1 in halves:
            add_terms(nc.vector, 0, v0, v1)
        nc.sync.dma_start(out[0:P, :], z[0][:])
        product(1, H, LOWER, 0)
        product(1, H, UPPER, 5)
        for v0, v1 in halves:
            gate_arg(1, 0, v0, v1)
        for v0, v1 in halves:
            squash(1, 0, v0, v1)
            fetch_passed(1, v0, v1)
        gate_arg(1, 1)
        squash(1, 1)
        for v0, v1 in halves:
            gated(1, 0, v0, v1)
        for v0, v1 in halves:
            times_gate(1, v0, v1)
        for queue, (v0, v1) in zip((nc.sync, nc.scalar), halves):
            add_terms(nc.vector, 1, v0, v1)
            queue.dma_start(out[P : 2 * P, v0:v1], z[1][:, v0:v1])
